import numpy as np
import ml_dtypes


def mxq(x, axis, fmt="e4m3"):
    dtype, down = {"e4m3": (ml_dtypes.float8_e4m3fn, 7), "e5m2": (ml_dtypes.float8_e5m2, 14)}[fmt]
    v = np.moveaxis(np.asarray(x, np.float32).astype(ml_dtypes.bfloat16).astype(np.float64), axis, -1)
    blocks = v.reshape(v.shape[:-1] + (-1, 32))
    amax = np.abs(blocks).max(-1, keepdims=True)
    byte = np.maximum(np.where(amax > 0, np.frexp(amax)[1] - 1 + 127, 0) - down, 1)
    scale = np.exp2(byte - 127.0)
    codes = (blocks / scale).astype(np.float32).astype(dtype).astype(np.float64)
    return np.moveaxis((codes * scale).reshape(v.shape), -1, axis)


WIDE = False


def mx_kscale(k):
    if not WIDE:
        return np.ones(k)
    levels = np.array([10, -10, 5, -5, 0])
    if k % 512:
        return np.exp2(np.random.permutation(np.resize(levels, k // 32))).repeat(32)
    a = np.empty((k // 512, 16))
    for p in range(k // 512):
        a[p, :8] = np.random.permutation(np.resize(levels, 8))
        for g in range(8):
            far = levels[np.abs(levels - a[p, g]) >= 10]
            a[p, g + 8] = far[np.random.randint(len(far))]
    return np.exp2(a.ravel()).repeat(32)


def f64(x):
    return np.asarray(x).astype(np.float64)


def striped(idx):
    return np.tile(idx.reshape(-1, 16).T, (8, 1)).astype(np.uint16)


def unstriped(offs):
    return offs[:16].T.reshape(-1).astype(np.int64)


def pack_weight(w):
    k, n = w.shape
    w = f64(np.asarray(w, np.float32).astype(ml_dtypes.bfloat16)).reshape(k // 32, 32, n)
    amax = np.abs(w).max(1)
    byte = np.clip(np.where(amax > 0, np.frexp(amax)[1] - 1 + 127 - 7, 1), 1, 254)
    scaled = (w * np.exp2(127.0 - byte)[:, None, :]).reshape(k, n).astype(np.float32)
    words = np.ascontiguousarray(scaled.reshape(k // 512, 128, 4, n).transpose(0, 1, 3, 2)).astype(ml_dtypes.float8_e4m3fn).view(np.uint8)
    return words, np.ascontiguousarray(byte.astype(np.uint8).reshape(k // 512, 16, n))


def unpack_weight(words, scales):
    g, p, n, _ = words.shape
    vals = np.ascontiguousarray(words).view(ml_dtypes.float8_e4m3fn).astype(np.float64) * np.repeat(np.exp2(scales.astype(np.float64) - 127.0), 8, axis=1)[..., None]
    return vals.transpose(0, 1, 3, 2).reshape(g * 512, n)


K, T, S, H, N = 512, 2048, 512, 512, 128


def setup_inputs():
    n = np.random.standard_normal
    s = mx_kscale(K)[:, None]
    u = mx_kscale(H)
    packed_w2 = pack_weight(n((H, N)) / np.sqrt(H) / u[:, None])
    return {
        "xT": (n((K, T)) * s).astype(np.float32),
        "w1": (n((K, H)) / np.sqrt(K) / s * u).astype(np.float32),
        "w2_words": packed_w2[0],
        "w2_scales": packed_w2[1],
        "pe": (0.5 * n((H, T)) * u[:, None]).astype(np.float32),
        "offs": striped(np.random.permutation(T)[:S]),
    }


def reference(xT, w1, w2_words, w2_scales, pe, offs):
    xq = mxq(f64(xT)[:, unstriped(offs)], 0, "e4m3")
    g = f64(pe)[:, unstriped(offs)]
    h = (mxq(f64(w1), 0, "e4m3").T @ xq) + g
    return unpack_weight(w2_words, w2_scales).T @ mxq(h, 0, "e4m3")

@@ -1,0 +1,119 @@
+from contextlib import ExitStack
+
+import concourse.mybir as mybir
+
+K, T, S, H, N = 512, 2048, 512, 512, 128
+FLOPS = 2 * K * H * S + 2 * H * N * S
+
+F32 = mybir.dt.float32
+BF16 = mybir.dt.bfloat16
+I32 = mybir.dt.int32
+U32 = mybir.dt.uint32
+U16 = mybir.dt.uint16
+U8 = mybir.dt.uint8
+FP8X4 = mybir.dt.float8_e4m3fn_x4
+ADD = mybir.AluOpType.add
+
+P = 128
+PACK = 4
+HALF = S // 2
+PART = S // 4
+
+
+def tile_picked_posadd_none_l_kernel(tc, xT, w1, w2_words, w2_scales, pe, offs, out):
+    nc = tc.nc
+    with ExitStack() as ctx:
+        sb = ctx.enter_context(tc.tile_pool(name="sb", bufs=1))
+        ps = ctx.enter_context(tc.psum_pool(name="ps", bufs=1))
+
+        def entries(first, count):
+            return offsets[:, first // 16 : (first + count) // 16]
+
+        offsets = sb.tile([P, S // 16], U16, name="offsets")
+        w1_raw = sb.tile([P, PACK, H], F32, name="w1_raw")
+        nc.sync.dma_start(w1_raw[:], w1.rearrange("(p j) c -> p j c", j=PACK))
+        nc.sync.dma_start(offsets[:], offs)
+
+        w2_codes = sb.tile([P, N], U32, name="w2_codes", align_bytes=64)
+        w2_sc = sb.tile([P, N], U8, name="w2_sc", align_bytes=64)
+        nc.vector.memset(w2_sc[:].bitcast(I32), 0)
+        nc.scalar.dma_start(w2_codes[:].bitcast(I32), w2_words[0].rearrange("p n t -> p (n t)").bitcast(I32))
+        for q in range(4):
+            nc.scalar.dma_start(w2_sc[32 * q : 32 * q + 4, :].bitcast(I32), w2_scales[0, 4 * q : 4 * q + 4, :].bitcast(I32))
+
+        x_rows = xT.rearrange("(p j) t -> j p t", j=PACK)
+        pe_rows = pe.rearrange("(p j) t -> j p t", j=PACK)
+        x_pl = [sb.tile([P, T], F32, name="x_pl%d" % j) for j in range(PACK)]
+        pe_pl = [sb.tile([P, T], F32, name="pe_pl%d" % j) for j in range(PACK)]
+        for j in range(PACK):
+            nc.sync.dma_start(x_pl[j][:], x_rows[j])
+        for j in range(PACK):
+            nc.sync.dma_start(pe_pl[j][:], pe_rows[j])
+
+        w1_bf = sb.tile([P, H * PACK], BF16, name="w1_bf", align_bytes=64)
+        nc.scalar.copy(
+            out=w1_bf[:].rearrange("p (t m j) -> p m j t", t=PACK, j=PACK),
+            in_=w1_raw[:].rearrange("p j (m t) -> p m j t", t=PACK),
+        )
+        w1_codes = sb.tile([P, H], U32, name="w1_codes", align_bytes=64)
+        w1_sc = sb.tile([P, H], U8, name="w1_sc", align_bytes=64)
+        nc.vector.quantize_mx(out=w1_codes[:].bitcast(FP8X4), scales=w1_sc[:], in_=w1_bf[:])
+
+        x_bf = [sb.tile([P, HALF, PACK], BF16, name="x_bf%d" % a, align_bytes=64) for a in range(2)]
+        x_codes = [sb.tile([P, HALF], U32, name="x_codes%d" % a, align_bytes=64) for a in range(2)]
+        x_sc = [sb.tile([P, HALF], U8, name="x_sc%d" % a, align_bytes=64) for a in range(2)]
+        for j in range(PACK):
+            for a in range(2):
+                nc.vector.tensor_copy(x_bf[a][:, :, j], x_pl[j][:].indirect(entries(a * HALF, HALF)))
+        prod = {}
+        for a in range(2):
+            nc.vector.quantize_mx(out=x_codes[a][:].bitcast(FP8X4), scales=x_sc[a][:], in_=x_bf[a][:].rearrange("p n j -> p (n j)"))
+            for u in range(2):
+                acc = ps.tile([P, 2, HALF], F32, name="acc%d%d" % (a, u))
+                for e in range(2):
+                    cols = slice((2 * u + e) * P, (2 * u + e + 1) * P)
+                    nc.tensor.matmul_mx(
+                        out=acc[:, e, :],
+                        lhsT=w1_codes[:, cols].bitcast(FP8X4),
+                        lhsT_scale=w1_sc[:, cols],
+                        rhs=x_codes[a][:].bitcast(FP8X4),
+                        rhs_scale=x_sc[a][:],
+                        start=True,
+                        stop=True,
+                    )
+                prod[a, u] = sb.tile([P, 2, HALF], F32, name="prod%d%d" % (a, u))
+                nc.scalar.copy(out=prod[a, u][:], in_=acc[:])
+
+        h_bf = [sb.tile([P, PART, PACK], BF16, name="h_bf%d" % c, align_bytes=64) for c in range(4)]
+        h_lo = [sb.tile([P, 2, HALF], F32, name="h_lo%d" % a) for a in range(2)]
+        for e in range(2):
+            for a in range(2):
+                nc.vector.tensor_tensor(h_lo[a][:, e, :], pe_pl[e][:].indirect(entries(a * HALF, HALF)), prod[a, 0][:, e, :], ADD)
+        for c in range(4):
+            a, n0 = divmod(c * PART, HALF)
+            nc.scalar.copy(out=h_bf[c][:, :, 0:2], in_=h_lo[a][:, :, n0 : n0 + PART].rearrange("p e n -> p n e"))
+
+        h_hi = [sb.tile([P, 2, PART], F32, name="h_hi%d" % c) for c in range(4)]
+        for e in range(2):
+            for c in range(4):
+                a, n0 = divmod(c * PART, HALF)
+                nc.vector.tensor_tensor(h_hi[c][:, e, :], pe_pl[2 + e][:].indirect(entries(c * PART, PART)), prod[a, 1][:, e, n0 : n0 + PART], ADD)
+        for c in range(4):
+            nc.scalar.copy(out=h_bf[c][:, :, 2:4], in_=h_hi[c][:].rearrange("p e n -> p n e"))
+        for c in range(4):
+            h_codes = sb.tile([P, PART], U32, name="h_codes%d" % c, align_bytes=64)
+            h_sc = sb.tile([P, PART], U8, name="h_sc%d" % c, align_bytes=64)
+            nc.vector.quantize_mx(out=h_codes[:].bitcast(FP8X4), scales=h_sc[:], in_=h_bf[c][:].rearrange("p n j -> p (n j)"))
+            res = ps.tile([P, PART], F32, name="res%d" % c)
+            nc.tensor.matmul_mx(
+                out=res[:],
+                lhsT=w2_codes[:].bitcast(FP8X4),
+                lhsT_scale=w2_sc[:],
+                rhs=h_codes[:].bitcast(FP8X4),
+                rhs_scale=h_sc[:],
+                start=True,
+                stop=True,
+            )
+            res_sb = sb.tile([P, PART], F32, name="res_sb%d" % c)
+            nc.scalar.copy(out=res_sb[:], in_=res[:])
+            nc.sync.dma_start(out[:, c * PART : (c + 1) * PART], res_sb[:])

@@ -37,9 +37,6 @@ def tile_picked_posadd_none_l_kernel(tc, xT, w1, w2_words, w2_scales, pe, offs, 
         w2_codes = sb.tile([P, N], U32, name="w2_codes", align_bytes=64)
         w2_sc = sb.tile([P, N], U8, name="w2_sc", align_bytes=64)
         nc.vector.memset(w2_sc[:].bitcast(I32), 0)
-        nc.scalar.dma_start(w2_codes[:].bitcast(I32), w2_words[0].rearrange("p n t -> p (n t)").bitcast(I32))
-        for q in range(4):
-            nc.scalar.dma_start(w2_sc[32 * q : 32 * q + 4, :].bitcast(I32), w2_scales[0, 4 * q : 4 * q + 4, :].bitcast(I32))
 
         x_rows = xT.rearrange("(p j) t -> j p t", j=PACK)
         pe_rows = pe.rearrange("(p j) t -> j p t", j=PACK)
@@ -49,6 +46,10 @@ def tile_picked_posadd_none_l_kernel(tc, xT, w1, w2_words, w2_scales, pe, offs, 
             nc.sync.dma_start(x_pl[j][:], x_rows[j])
         for j in range(PACK):
             nc.sync.dma_start(pe_pl[j][:], pe_rows[j])
+        nc.sync.dma_start(w2_codes[:].bitcast(I32), w2_words[0].rearrange("p n t -> p (n t)").bitcast(I32))
+        for q in range(4):
+            nc.sync.dma_start(w2_sc[32 * q : 32 * q + 4, :].bitcast(I32), w2_scales[0, 4 * q : 4 * q + 4, :].bitcast(I32))
+
 
         w1_bf = sb.tile([P, H * PACK], BF16, name="w1_bf", align_bytes=64)
         nc.scalar.copy(

@@ -17,7 +17,8 @@ ADD = mybir.AluOpType.add
 P = 128
 PACK = 4
 HALF = S // 2
-PART = S // 4
+CHUNKS = (128, 128, 128, 128,)
+VCAST = ()
 
 
 def tile_picked_posadd_none_l_kernel(tc, xT, w1, w2_words, w2_scales, pe, offs, out):
@@ -31,52 +32,55 @@ def tile_picked_posadd_none_l_kernel(tc, xT, w1, w2_words, w2_scales, pe, offs, 
 
         offsets = sb.tile([P, S // 16], U16, name="offsets")
         w1_raw = sb.tile([P, PACK, H], F32, name="w1_raw")
-        nc.sync.dma_start(w1_raw[:], w1.rearrange("(p j) c -> p j c", j=PACK))
-        nc.sync.dma_start(offsets[:], offs)
-
         w2_codes = sb.tile([P, N], U32, name="w2_codes", align_bytes=64)
         w2_sc = sb.tile([P, N], U8, name="w2_sc", align_bytes=64)
         nc.vector.memset(w2_sc[:].bitcast(I32), 0)
+        nc.scalar.dma_start(w2_codes[:].bitcast(I32), w2_words[0].rearrange("p n t -> p (n t)").bitcast(I32))
+        for q in range(4):
+            nc.scalar.dma_start(w2_sc[32 * q : 32 * q + 4, :].bitcast(I32), w2_scales[0, 4 * q : 4 * q + 4, :].bitcast(I32))
 
-        x_rows = xT.rearrange("(p j) t -> j p t", j=PACK)
+        x_rows = xT.rearrange("(p u e) t -> u p e t", u=2, e=2)
         pe_rows = pe.rearrange("(p j) t -> j p t", j=PACK)
-        x_pl = [sb.tile([P, T], F32, name="x_pl%d" % j) for j in range(PACK)]
+        x_pr = [sb.tile([P, 2, T], F32, name="x_pr%d" % u) for u in range(2)]
         pe_pl = [sb.tile([P, T], F32, name="pe_pl%d" % j) for j in range(PACK)]
-        for j in range(PACK):
-            nc.sync.dma_start(x_pl[j][:], x_rows[j])
+        nc.sync.dma_start(x_pr[0][:], x_rows[0])
+        nc.sync.dma_start(offsets[:], offs)
+        nc.sync.dma_start(x_pr[1][:], x_rows[1])
+        nc.sync.dma_start(w1_raw[:], w1.rearrange("(p j) c -> p j c", j=PACK))
         for j in range(PACK):
             nc.sync.dma_start(pe_pl[j][:], pe_rows[j])
-        nc.sync.dma_start(w2_codes[:].bitcast(I32), w2_words[0].rearrange("p n t -> p (n t)").bitcast(I32))
-        for q in range(4):
-            nc.sync.dma_start(w2_sc[32 * q : 32 * q + 4, :].bitcast(I32), w2_scales[0, 4 * q : 4 * q + 4, :].bitcast(I32))
-
-
-        w1_bf = sb.tile([P, H * PACK], BF16, name="w1_bf", align_bytes=64)
-        nc.scalar.copy(
-            out=w1_bf[:].rearrange("p (t m j) -> p m j t", t=PACK, j=PACK),
-            in_=w1_raw[:].rearrange("p j (m t) -> p m j t", t=PACK),
-        )
-        w1_codes = sb.tile([P, H], U32, name="w1_codes", align_bytes=64)
-        w1_sc = sb.tile([P, H], U8, name="w1_sc", align_bytes=64)
-        nc.vector.quantize_mx(out=w1_codes[:].bitcast(FP8X4), scales=w1_sc[:], in_=w1_bf[:])
 
         x_bf = [sb.tile([P, HALF, PACK], BF16, name="x_bf%d" % a, align_bytes=64) for a in range(2)]
         x_codes = [sb.tile([P, HALF], U32, name="x_codes%d" % a, align_bytes=64) for a in range(2)]
         x_sc = [sb.tile([P, HALF], U8, name="x_sc%d" % a, align_bytes=64) for a in range(2)]
-        for j in range(PACK):
+        for u in range(2):
             for a in range(2):
-                nc.vector.tensor_copy(x_bf[a][:, :, j], x_pl[j][:].indirect(entries(a * HALF, HALF)))
-        prod = {}
+                for e in range(2):
+                    nc.vector.tensor_copy(x_bf[a][:, :, 2 * u + e], x_pr[u][:, e, :].indirect(entries(a * HALF, HALF)))
         for a in range(2):
             nc.vector.quantize_mx(out=x_codes[a][:].bitcast(FP8X4), scales=x_sc[a][:], in_=x_bf[a][:].rearrange("p n j -> p (n j)"))
-            for u in range(2):
-                acc = ps.tile([P, 2, HALF], F32, name="acc%d%d" % (a, u))
+
+        w1_codes, w1_sc = [], []
+        for u in range(2):
+            w1_bf = sb.tile([P, 2 * P * PACK], BF16, name="w1_bf%d" % u, align_bytes=64)
+            nc.scalar.copy(
+                out=w1_bf[:].rearrange("p (e m j) -> p m j e", e=2, j=PACK),
+                in_=w1_raw[:].rearrange("p j (m t) -> p m j t", t=PACK)[:, :, :, 2 * u : 2 * u + 2],
+            )
+            w1_codes.append(sb.tile([P, 2 * P], U32, name="w1_codes%d" % u, align_bytes=64))
+            w1_sc.append(sb.tile([P, 2 * P], U8, name="w1_sc%d" % u, align_bytes=64))
+            nc.vector.quantize_mx(out=w1_codes[u][:].bitcast(FP8X4), scales=w1_sc[u][:], in_=w1_bf[:])
+
+        prod = {}
+        for u in range(2):
+            for a in range(2):
+                acc = ps.tile([P, 2, HALF], F32, name="acc%d%d" % (u, a))
                 for e in range(2):
-                    cols = slice((2 * u + e) * P, (2 * u + e + 1) * P)
+                    cols = slice(e * P, (e + 1) * P)
                     nc.tensor.matmul_mx(
                         out=acc[:, e, :],
-                        lhsT=w1_codes[:, cols].bitcast(FP8X4),
-                        lhsT_scale=w1_sc[:, cols],
+                        lhsT=w1_codes[u][:, cols].bitcast(FP8X4),
+                        lhsT_scale=w1_sc[u][:, cols],
                         rhs=x_codes[a][:].bitcast(FP8X4),
                         rhs_scale=x_sc[a][:],
                         start=True,
@@ -85,27 +89,31 @@ def tile_picked_posadd_none_l_kernel(tc, xT, w1, w2_words, w2_scales, pe, offs, 
                 prod[a, u] = sb.tile([P, 2, HALF], F32, name="prod%d%d" % (a, u))
                 nc.scalar.copy(out=prod[a, u][:], in_=acc[:])
 
-        h_bf = [sb.tile([P, PART, PACK], BF16, name="h_bf%d" % c, align_bytes=64) for c in range(4)]
+        starts = [sum(CHUNKS[:c]) for c in range(len(CHUNKS))]
+        h_bf = [sb.tile([P, n, PACK], BF16, name="h_bf%d" % c, align_bytes=64) for c, n in enumerate(CHUNKS)]
         h_lo = [sb.tile([P, 2, HALF], F32, name="h_lo%d" % a) for a in range(2)]
         for e in range(2):
             for a in range(2):
                 nc.vector.tensor_tensor(h_lo[a][:, e, :], pe_pl[e][:].indirect(entries(a * HALF, HALF)), prod[a, 0][:, e, :], ADD)
-        for c in range(4):
-            a, n0 = divmod(c * PART, HALF)
-            nc.scalar.copy(out=h_bf[c][:, :, 0:2], in_=h_lo[a][:, :, n0 : n0 + PART].rearrange("p e n -> p n e"))
+        for c, n in enumerate(CHUNKS):
+            a, n0 = divmod(starts[c], HALF)
+            nc.scalar.copy(out=h_bf[c][:, :, 0:2], in_=h_lo[a][:, :, n0 : n0 + n].rearrange("p e n -> p n e"))
 
-        h_hi = [sb.tile([P, 2, PART], F32, name="h_hi%d" % c) for c in range(4)]
+        h_hi = [sb.tile([P, 2, n], F32, name="h_hi%d" % c) for c, n in enumerate(CHUNKS)]
         for e in range(2):
-            for c in range(4):
-                a, n0 = divmod(c * PART, HALF)
-                nc.vector.tensor_tensor(h_hi[c][:, e, :], pe_pl[2 + e][:].indirect(entries(c * PART, PART)), prod[a, 1][:, e, n0 : n0 + PART], ADD)
-        for c in range(4):
-            nc.scalar.copy(out=h_bf[c][:, :, 2:4], in_=h_hi[c][:].rearrange("p e n -> p n e"))
-        for c in range(4):
-            h_codes = sb.tile([P, PART], U32, name="h_codes%d" % c, align_bytes=64)
-            h_sc = sb.tile([P, PART], U8, name="h_sc%d" % c, align_bytes=64)
+            for c, n in enumerate(CHUNKS):
+                a, n0 = divmod(starts[c], HALF)
+                nc.vector.tensor_tensor(h_hi[c][:, e, :], pe_pl[2 + e][:].indirect(entries(starts[c], n)), prod[a, 1][:, e, n0 : n0 + n], ADD)
+        for c, n in enumerate(CHUNKS):
+            if c in VCAST:
+                nc.vector.tensor_copy(h_bf[c][:, :, 2:4], h_hi[c][:].rearrange("p e n -> p n e"))
+            else:
+                nc.scalar.copy(out=h_bf[c][:, :, 2:4], in_=h_hi[c][:].rearrange("p e n -> p n e"))
+        for c, n in enumerate(CHUNKS):
+            h_codes = sb.tile([P, n], U32, name="h_codes%d" % c, align_bytes=64)
+            h_sc = sb.tile([P, n], U8, name="h_sc%d" % c, align_bytes=64)
             nc.vector.quantize_mx(out=h_codes[:].bitcast(FP8X4), scales=h_sc[:], in_=h_bf[c][:].rearrange("p n j -> p (n j)"))
-            res = ps.tile([P, PART], F32, name="res%d" % c)
+            res = ps.tile([P, n], F32, name="res%d" % c)
             nc.tensor.matmul_mx(
                 out=res[:],
                 lhsT=w2_codes[:].bitcast(FP8X4),
@@ -115,6 +123,6 @@ def tile_picked_posadd_none_l_kernel(tc, xT, w1, w2_words, w2_scales, pe, offs, 
                 start=True,
                 stop=True,
             )
-            res_sb = sb.tile([P, PART], F32, name="res_sb%d" % c)
+            res_sb = sb.tile([P, n], F32, name="res_sb%d" % c)
             nc.scalar.copy(out=res_sb[:], in_=res[:])
-            nc.sync.dma_start(out[:, c * PART : (c + 1) * PART], res_sb[:])
+            nc.sync.dma_start(out[:, starts[c] : starts[c] + n], res_sb[:])

@@ -17,8 +17,7 @@ ADD = mybir.AluOpType.add
 P = 128
 PACK = 4
 HALF = S // 2
-CHUNKS = (128, 128, 128, 128,)
-VCAST = ()
+CHUNKS = (128, 128, 128, 64, 64,)
 
 
 def tile_picked_posadd_none_l_kernel(tc, xT, w1, w2_words, w2_scales, pe, offs, out):
@@ -71,7 +70,7 @@ def tile_picked_posadd_none_l_kernel(tc, xT, w1, w2_words, w2_scales, pe, offs, 
             w1_sc.append(sb.tile([P, 2 * P], U8, name="w1_sc%d" % u, align_bytes=64))
             nc.vector.quantize_mx(out=w1_codes[u][:].bitcast(FP8X4), scales=w1_sc[u][:], in_=w1_bf[:])
 
-        prod = {}
+        prod = [sb.tile([P, S], F32, name="prod%d" % t) for t in range(PACK)]
         for u in range(2):
             for a in range(2):
                 acc = ps.tile([P, 2, HALF], F32, name="acc%d%d" % (u, a))
@@ -86,36 +85,41 @@ def tile_picked_posadd_none_l_kernel(tc, xT, w1, w2_words, w2_scales, pe, offs, 
                         start=True,
                         stop=True,
                     )
-                prod[a, u] = sb.tile([P, 2, HALF], F32, name="prod%d%d" % (a, u))
-                nc.scalar.copy(out=prod[a, u][:], in_=acc[:])
+                nc.scalar.copy(out=prod[2 * u][:, a * HALF : (a + 1) * HALF], in_=acc[:, 0, :])
+                nc.scalar.copy(out=prod[2 * u + 1][:, a * HALF : (a + 1) * HALF], in_=acc[:, 1, :])
 
         starts = [sum(CHUNKS[:c]) for c in range(len(CHUNKS))]
-        h_bf = [sb.tile([P, n, PACK], BF16, name="h_bf%d" % c, align_bytes=64) for c, n in enumerate(CHUNKS)]
-        h_lo = [sb.tile([P, 2, HALF], F32, name="h_lo%d" % a) for a in range(2)]
+        last = len(CHUNKS) - 1
+        early = starts[last]
+        h_bf = [sb.tile([P, n, PACK], BF16, name="h_bf%d" % c, align_bytes=64) for c, n in enumerate(CHUNKS[:last])]
+        h_lo = sb.tile([P, 2, early], F32, name="h_lo")
+        h_last = sb.tile([P, PACK, CHUNKS[last]], F32, name="h_last")
         for e in range(2):
-            for a in range(2):
-                nc.vector.tensor_tensor(h_lo[a][:, e, :], pe_pl[e][:].indirect(entries(a * HALF, HALF)), prod[a, 0][:, e, :], ADD)
-        for c, n in enumerate(CHUNKS):
-            a, n0 = divmod(starts[c], HALF)
-            nc.scalar.copy(out=h_bf[c][:, :, 0:2], in_=h_lo[a][:, :, n0 : n0 + n].rearrange("p e n -> p n e"))
+            for lo, hi in ((0, HALF), (HALF, early)):
+                nc.vector.tensor_tensor(h_lo[:, e, lo:hi], pe_pl[e][:].indirect(entries(lo, hi - lo)), prod[e][:, lo:hi], ADD)
+            nc.vector.tensor_tensor(h_last[:, e, :], pe_pl[e][:].indirect(entries(early, S - early)), prod[e][:, early:S], ADD)
+        for c, n in enumerate(CHUNKS[:last]):
+            nc.scalar.copy(out=h_bf[c][:, :, 0:2], in_=h_lo[:, :, starts[c] : starts[c] + n].rearrange("p e n -> p n e"))
 
-        h_hi = [sb.tile([P, 2, n], F32, name="h_hi%d" % c) for c, n in enumerate(CHUNKS)]
+        h_hi = [sb.tile([P, 2, n], F32, name="h_hi%d" % c) for c, n in enumerate(CHUNKS[:last])]
         for e in range(2):
             for c, n in enumerate(CHUNKS):
-                a, n0 = divmod(starts[c], HALF)
-                nc.vector.tensor_tensor(h_hi[c][:, e, :], pe_pl[2 + e][:].indirect(entries(starts[c], n)), prod[a, 1][:, e, n0 : n0 + n], ADD)
+                dst = h_hi[c][:, e, :] if c < last else h_last[:, 2 + e, :]
+                nc.vector.tensor_tensor(dst, pe_pl[2 + e][:].indirect(entries(starts[c], n)), prod[2 + e][:, starts[c] : starts[c] + n], ADD)
+        for c, n in enumerate(CHUNKS[:last]):
+            nc.scalar.copy(out=h_bf[c][:, :, 2:4], in_=h_hi[c][:].rearrange("p e n -> p n e"))
+        res_sb = sb.tile([P, S], F32, name="res_sb")
+        first_of = {1: 0, 4: 2}
         for c, n in enumerate(CHUNKS):
-            if c in VCAST:
-                nc.vector.tensor_copy(h_bf[c][:, :, 2:4], h_hi[c][:].rearrange("p e n -> p n e"))
-            else:
-                nc.scalar.copy(out=h_bf[c][:, :, 2:4], in_=h_hi[c][:].rearrange("p e n -> p n e"))
-        for c, n in enumerate(CHUNKS):
-            h_codes = sb.tile([P, n], U32, name="h_codes%d" % c, align_bytes=64)
+            if c == 2:
+                h_bf.append(sb.tile([P, CHUNKS[last], PACK], BF16, name="h_bf_last", tag="h_bf0", align_bytes=64))
+                nc.vector.tensor_copy(h_bf[last][:], h_last[:].rearrange("p t n -> p n t"))
+            h_codes = sb.tile([P, n], U32, name="h_codes%d" % c, tag="h_codes%d" % (c % last), align_bytes=64)
             h_sc = sb.tile([P, n], U8, name="h_sc%d" % c, align_bytes=64)
             nc.vector.quantize_mx(out=h_codes[:].bitcast(FP8X4), scales=h_sc[:], in_=h_bf[c][:].rearrange("p n j -> p (n j)"))
-            res = ps.tile([P, n], F32, name="res%d" % c)
+            res = ps.tile([P, 2, HALF], F32, name="res%d" % c, tag="res%d" % c if c < 4 else "acc0%d" % (c - 4))[:, 0, 0:n]
             nc.tensor.matmul_mx(
-                out=res[:],
+                out=res,
                 lhsT=w2_codes[:].bitcast(FP8X4),
                 lhsT_scale=w2_sc[:],
                 rhs=h_codes[:].bitcast(FP8X4),
@@ -123,6 +127,10 @@ def tile_picked_posadd_none_l_kernel(tc, xT, w1, w2_words, w2_scales, pe, offs, 
                 start=True,
                 stop=True,
             )
-            res_sb = sb.tile([P, n], F32, name="res_sb%d" % c)
-            nc.scalar.copy(out=res_sb[:], in_=res[:])
-            nc.sync.dma_start(out[:, starts[c] : starts[c] + n], res_sb[:])
+            if c in (3, 4,):
+                nc.vector.tensor_copy(res_sb[:, starts[c] : starts[c] + n], res)
+            else:
+                nc.scalar.copy(out=res_sb[:, starts[c] : starts[c] + n], in_=res)
+            if c in first_of:
+                cols = slice(starts[first_of[c]], starts[c] + n)
+                nc.sync.dma_start(out[:, cols], res_sb[:, cols])

@@ -17,7 +17,12 @@ ADD = mybir.AluOpType.add
 P = 128
 PACK = 4
 HALF = S // 2
-CHUNKS = (128, 128, 128, 64, 64,)
+PIECE = 128
+CHUNKS = (128, 128, 128, 64, 64)
+STARTS = tuple(sum(CHUNKS[:c]) for c in range(len(CHUNKS) + 1))
+LAST = len(CHUNKS) - 1
+FIRST_ON_VECTOR = 3
+LINE = 4
 
 
 def tile_picked_posadd_none_l_kernel(tc, xT, w1, w2_words, w2_scales, pe, offs, out):
@@ -26,11 +31,9 @@ def tile_picked_posadd_none_l_kernel(tc, xT, w1, w2_words, w2_scales, pe, offs, 
         sb = ctx.enter_context(tc.tile_pool(name="sb", bufs=1))
         ps = ctx.enter_context(tc.psum_pool(name="ps", bufs=1))
 
-        def entries(first, count):
-            return offsets[:, first // 16 : (first + count) // 16]
-
         offsets = sb.tile([P, S // 16], U16, name="offsets")
         w1_raw = sb.tile([P, PACK, H], F32, name="w1_raw")
+
         w2_codes = sb.tile([P, N], U32, name="w2_codes", align_bytes=64)
         w2_sc = sb.tile([P, N], U8, name="w2_sc", align_bytes=64)
         nc.vector.memset(w2_sc[:].bitcast(I32), 0)
@@ -39,25 +42,28 @@ def tile_picked_posadd_none_l_kernel(tc, xT, w1, w2_words, w2_scales, pe, offs, 
             nc.scalar.dma_start(w2_sc[32 * q : 32 * q + 4, :].bitcast(I32), w2_scales[0, 4 * q : 4 * q + 4, :].bitcast(I32))
 
         x_rows = xT.rearrange("(p u e) t -> u p e t", u=2, e=2)
-        pe_rows = pe.rearrange("(p j) t -> j p t", j=PACK)
-        x_pr = [sb.tile([P, 2, T], F32, name="x_pr%d" % u) for u in range(2)]
-        pe_pl = [sb.tile([P, T], F32, name="pe_pl%d" % j) for j in range(PACK)]
-        nc.sync.dma_start(x_pr[0][:], x_rows[0])
+        pe_rows = pe.rearrange("(p t) c -> t p c", t=PACK)
+        x_pair = [sb.tile([P, 2, T], F32, name="x_pair%d" % u) for u in range(2)]
+        pe_plane = [sb.tile([P, T], F32, name="pe_plane%d" % t) for t in range(PACK)]
+        nc.sync.dma_start(x_pair[0][:], x_rows[0])
         nc.sync.dma_start(offsets[:], offs)
-        nc.sync.dma_start(x_pr[1][:], x_rows[1])
+        nc.sync.dma_start(x_pair[1][:], x_rows[1])
         nc.sync.dma_start(w1_raw[:], w1.rearrange("(p j) c -> p j c", j=PACK))
-        for j in range(PACK):
-            nc.sync.dma_start(pe_pl[j][:], pe_rows[j])
+        for t in range(PACK):
+            nc.sync.dma_start(pe_plane[t][:], pe_rows[t])
 
-        x_bf = [sb.tile([P, HALF, PACK], BF16, name="x_bf%d" % a, align_bytes=64) for a in range(2)]
+        x_bf = sb.tile([P, S, PACK], BF16, name="x_bf", align_bytes=64)
+        for u in range(2):
+            for e in range(2):
+                nc.vector.tensor_copy(x_bf[:, :, 2 * u + e], x_pair[u][:, e, :].indirect(offsets[:]))
         x_codes = [sb.tile([P, HALF], U32, name="x_codes%d" % a, align_bytes=64) for a in range(2)]
         x_sc = [sb.tile([P, HALF], U8, name="x_sc%d" % a, align_bytes=64) for a in range(2)]
-        for u in range(2):
-            for a in range(2):
-                for e in range(2):
-                    nc.vector.tensor_copy(x_bf[a][:, :, 2 * u + e], x_pr[u][:, e, :].indirect(entries(a * HALF, HALF)))
         for a in range(2):
-            nc.vector.quantize_mx(out=x_codes[a][:].bitcast(FP8X4), scales=x_sc[a][:], in_=x_bf[a][:].rearrange("p n j -> p (n j)"))
+            nc.vector.quantize_mx(
+                out=x_codes[a][:].bitcast(FP8X4),
+                scales=x_sc[a][:],
+                in_=x_bf[:, a * HALF : (a + 1) * HALF, :].rearrange("p n j -> p (n j)"),
+            )
 
         w1_codes, w1_sc = [], []
         for u in range(2):
@@ -71,55 +77,60 @@ def tile_picked_posadd_none_l_kernel(tc, xT, w1, w2_words, w2_scales, pe, offs, 
             nc.vector.quantize_mx(out=w1_codes[u][:].bitcast(FP8X4), scales=w1_sc[u][:], in_=w1_bf[:])
 
         prod = [sb.tile([P, S], F32, name="prod%d" % t) for t in range(PACK)]
-        for u in range(2):
+        for t in (0, 1, 3, 2):
+            u, e = divmod(t, 2)
+            w1_cols = slice(e * P, (e + 1) * P)
             for a in range(2):
-                acc = ps.tile([P, 2, HALF], F32, name="acc%d%d" % (u, a))
-                for e in range(2):
-                    cols = slice(e * P, (e + 1) * P)
-                    nc.tensor.matmul_mx(
-                        out=acc[:, e, :],
-                        lhsT=w1_codes[u][:, cols].bitcast(FP8X4),
-                        lhsT_scale=w1_sc[u][:, cols],
-                        rhs=x_codes[a][:].bitcast(FP8X4),
-                        rhs_scale=x_sc[a][:],
-                        start=True,
-                        stop=True,
-                    )
-                nc.scalar.copy(out=prod[2 * u][:, a * HALF : (a + 1) * HALF], in_=acc[:, 0, :])
-                nc.scalar.copy(out=prod[2 * u + 1][:, a * HALF : (a + 1) * HALF], in_=acc[:, 1, :])
+                acc = ps.tile([P, HALF], F32, name="acc%d%d" % (t, a), tag="bank%d" % (2 * t + a))
+                nc.tensor.matmul_mx(
+                    out=acc[:],
+                    lhsT=w1_codes[u][:, w1_cols].bitcast(FP8X4),
+                    lhsT_scale=w1_sc[u][:, w1_cols],
+                    rhs=x_codes[a][:].bitcast(FP8X4),
+                    rhs_scale=x_sc[a][:],
+                    start=True,
+                    stop=True,
+                )
+                nc.scalar.copy(out=prod[t][:, a * HALF : (a + 1) * HALF], in_=acc[:])
 
-        starts = [sum(CHUNKS[:c]) for c in range(len(CHUNKS))]
-        last = len(CHUNKS) - 1
-        early = starts[last]
-        h_bf = [sb.tile([P, n, PACK], BF16, name="h_bf%d" % c, align_bytes=64) for c, n in enumerate(CHUNKS[:last])]
-        h_lo = sb.tile([P, 2, early], F32, name="h_lo")
-        h_last = sb.tile([P, PACK, CHUNKS[last]], F32, name="h_last")
-        for e in range(2):
-            for lo, hi in ((0, HALF), (HALF, early)):
-                nc.vector.tensor_tensor(h_lo[:, e, lo:hi], pe_pl[e][:].indirect(entries(lo, hi - lo)), prod[e][:, lo:hi], ADD)
-            nc.vector.tensor_tensor(h_last[:, e, :], pe_pl[e][:].indirect(entries(early, S - early)), prod[e][:, early:S], ADD)
-        for c, n in enumerate(CHUNKS[:last]):
-            nc.scalar.copy(out=h_bf[c][:, :, 0:2], in_=h_lo[:, :, starts[c] : starts[c] + n].rearrange("p e n -> p n e"))
+        h = sb.tile([P, PACK, S], F32, name="h")
+        h_bf = [sb.tile([P, n, PACK], BF16, name="h_bf%d" % c, align_bytes=64) for c, n in enumerate(CHUNKS[:LAST])]
 
-        h_hi = [sb.tile([P, 2, n], F32, name="h_hi%d" % c) for c, n in enumerate(CHUNKS[:last])]
-        for e in range(2):
-            for c, n in enumerate(CHUNKS):
-                dst = h_hi[c][:, e, :] if c < last else h_last[:, 2 + e, :]
-                nc.vector.tensor_tensor(dst, pe_pl[2 + e][:].indirect(entries(starts[c], n)), prod[2 + e][:, starts[c] : starts[c] + n], ADD)
-        for c, n in enumerate(CHUNKS[:last]):
-            nc.scalar.copy(out=h_bf[c][:, :, 2:4], in_=h_hi[c][:].rearrange("p e n -> p n e"))
+        def round_pair_on_scalar(c, t):
+            nc.scalar.copy(out=h_bf[c][:, :, t : t + 2], in_=h[:, t : t + 2, STARTS[c] : STARTS[c + 1]].rearrange("p e n -> p n e"))
+
+        def gather_and_add(t, first, count):
+            piece = slice(first, first + count)
+            picked = pe_plane[t][:].indirect(offsets[:, first // 16 : (first + count) // 16])
+            nc.vector.tensor_tensor(h[:, t, piece], picked, prod[t][:, piece], ADD)
+
+        gather_and_add(0, 0, S)
+        gather_and_add(1, 0, S)
+        for c in range(LAST):
+            round_pair_on_scalar(c, 0)
+        gather_and_add(2, 0, S)
+        for c in range(LAST):
+            gather_and_add(3, c * PIECE, PIECE)
+            round_pair_on_scalar(c, 2)
+
         res_sb = sb.tile([P, S], F32, name="res_sb")
-        first_of = {1: 0, 4: 2}
-        for c, n in enumerate(CHUNKS):
-            if c == 2:
-                h_bf.append(sb.tile([P, CHUNKS[last], PACK], BF16, name="h_bf_last", tag="h_bf0", align_bytes=64))
-                nc.vector.tensor_copy(h_bf[last][:], h_last[:].rearrange("p t n -> p n t"))
-            h_codes = sb.tile([P, n], U32, name="h_codes%d" % c, tag="h_codes%d" % (c % last), align_bytes=64)
+
+        def round_last_chunk_on_vector():
+            tile = sb.tile([P, CHUNKS[LAST], PACK], BF16, name="h_bf_last", tag="h_bf0", align_bytes=64)
+            nc.vector.tensor_copy(
+                tile[:].rearrange("p (g i) t -> p g t i", i=LINE),
+                h[:, :, STARTS[LAST] : S].rearrange("p t (g i) -> p g t i", i=LINE),
+            )
+            h_bf.append(tile)
+
+        def second_product(c):
+            n = CHUNKS[c]
+            h_codes = sb.tile([P, n], U32, name="h_codes%d" % c, tag="h_codes%d" % (c % LAST), align_bytes=64)
             h_sc = sb.tile([P, n], U8, name="h_sc%d" % c, align_bytes=64)
-            nc.vector.quantize_mx(out=h_codes[:].bitcast(FP8X4), scales=h_sc[:], in_=h_bf[c][:].rearrange("p n j -> p (n j)"))
-            res = ps.tile([P, 2, HALF], F32, name="res%d" % c, tag="res%d" % c if c < 4 else "acc0%d" % (c - 4))[:, 0, 0:n]
+            nc.vector.quantize_mx(out=h_codes[:].bitcast(FP8X4), scales=h_sc[:], in_=h_bf[c][:].rearrange("p n t -> p (n t)"))
+            res = ps.tile([P, n], F32, name="res%d" % c, tag="bank%d" % c)
             nc.tensor.matmul_mx(
-                out=res,
+                out=res[:],
                 lhsT=w2_codes[:].bitcast(FP8X4),
                 lhsT_scale=w2_sc[:],
                 rhs=h_codes[:].bitcast(FP8X4),
@@ -127,10 +138,21 @@ def tile_picked_posadd_none_l_kernel(tc, xT, w1, w2_words, w2_scales, pe, offs, 
                 start=True,
                 stop=True,
             )
-            if c in (3, 4,):
-                nc.vector.tensor_copy(res_sb[:, starts[c] : starts[c] + n], res)
+            if c >= FIRST_ON_VECTOR:
+                nc.vector.tensor_copy(res_sb[:, STARTS[c] : STARTS[c + 1]], res[:])
             else:
-                nc.scalar.copy(out=res_sb[:, starts[c] : starts[c] + n], in_=res)
-            if c in first_of:
-                cols = slice(starts[first_of[c]], starts[c] + n)
-                nc.sync.dma_start(out[:, cols], res_sb[:, cols])
+                nc.scalar.copy(out=res_sb[:, STARTS[c] : STARTS[c + 1]], in_=res[:])
+
+        def store(queue, first_chunk, last_chunk):
+            out_cols = slice(STARTS[first_chunk], STARTS[last_chunk + 1])
+            queue.dma_start(out[:, out_cols], res_sb[:, out_cols])
+
+        second_product(0)
+        second_product(1)
+        store(nc.sync, 0, 1)
+        round_last_chunk_on_vector()
+        second_product(2)
+        store(nc.scalar, 2, 2)
+        second_product(3)
+        second_product(LAST)
+        store(nc.sync, FIRST_ON_VECTOR, LAST)

@@ -76,7 +76,10 @@ def tile_picked_posadd_none_l_kernel(tc, xT, w1, w2_words, w2_scales, pe, offs, 
             w1_sc.append(sb.tile([P, 2 * P], U8, name="w1_sc%d" % u, align_bytes=64))
             nc.vector.quantize_mx(out=w1_codes[u][:].bitcast(FP8X4), scales=w1_sc[u][:], in_=w1_bf[:])
 
-        prod = [sb.tile([P, S], F32, name="prod%d" % t) for t in range(PACK)]
+        prod = [None] + [sb.tile([P, S], F32, name="prod%d" % t) for t in range(1, PACK)]
+        h = sb.tile([P, PACK, S], F32, name="h", tag="w1_bf1", align_bytes=64)
+        picked0 = sb.tile([P, S], F32, name="picked0", tag="w1_bf0", align_bytes=64)
+        nc.vector.tensor_copy(picked0[:], pe_plane[0][:].indirect(offsets[:]))
         for t in (0, 1, 3, 2):
             u, e = divmod(t, 2)
             w1_cols = slice(e * P, (e + 1) * P)
@@ -91,9 +94,12 @@ def tile_picked_posadd_none_l_kernel(tc, xT, w1, w2_words, w2_scales, pe, offs, 
                     start=True,
                     stop=True,
                 )
-                nc.scalar.copy(out=prod[t][:, a * HALF : (a + 1) * HALF], in_=acc[:])
+                cols = slice(a * HALF, (a + 1) * HALF)
+                if t == 0:
+                    nc.vector.tensor_tensor(h[:, 0, cols], picked0[:, cols], acc[:], ADD)
+                else:
+                    nc.scalar.copy(out=prod[t][:, cols], in_=acc[:])
 
-        h = sb.tile([P, PACK, S], F32, name="h")
         h_bf = [sb.tile([P, n, PACK], BF16, name="h_bf%d" % c, align_bytes=64) for c, n in enumerate(CHUNKS[:LAST])]
 
         def round_pair_on_scalar(c, t):
@@ -104,7 +110,6 @@ def tile_picked_posadd_none_l_kernel(tc, xT, w1, w2_words, w2_scales, pe, offs, 
             picked = pe_plane[t][:].indirect(offsets[:, first // 16 : (first + count) // 16])
             nc.vector.tensor_tensor(h[:, t, piece], picked, prod[t][:, piece], ADD)
 
-        gather_and_add(0, 0, S)
         gather_and_add(1, 0, S)
         for c in range(LAST):
             round_pair_on_scalar(c, 0)

@@ -22,7 +22,6 @@ CHUNKS = (128, 128, 128, 64, 64)
 STARTS = tuple(sum(CHUNKS[:c]) for c in range(len(CHUNKS) + 1))
 LAST = len(CHUNKS) - 1
 FIRST_ON_VECTOR = 3
-LINE = 4
 
 
 def tile_picked_posadd_none_l_kernel(tc, xT, w1, w2_words, w2_scales, pe, offs, out):
@@ -100,10 +99,10 @@ def tile_picked_posadd_none_l_kernel(tc, xT, w1, w2_words, w2_scales, pe, offs, 
                 else:
                     nc.scalar.copy(out=prod[t][:, cols], in_=acc[:])
 
-        h_bf = [sb.tile([P, n, PACK], BF16, name="h_bf%d" % c, align_bytes=64) for c, n in enumerate(CHUNKS[:LAST])]
+        h_bf = sb.tile([P, S, PACK], BF16, name="h_bf", align_bytes=64)
 
-        def round_pair_on_scalar(c, t):
-            nc.scalar.copy(out=h_bf[c][:, :, t : t + 2], in_=h[:, t : t + 2, STARTS[c] : STARTS[c + 1]].rearrange("p e n -> p n e"))
+        def round_pair(copy, t, first, stop):
+            copy(h_bf[:, first:stop, t : t + 2], h[:, t : t + 2, first:stop].rearrange("p e n -> p n e"))
 
         def gather_and_add(t, first, count):
             piece = slice(first, first + count)
@@ -111,28 +110,24 @@ def tile_picked_posadd_none_l_kernel(tc, xT, w1, w2_words, w2_scales, pe, offs, 
             nc.vector.tensor_tensor(h[:, t, piece], picked, prod[t][:, piece], ADD)
 
         gather_and_add(1, 0, S)
-        for c in range(LAST):
-            round_pair_on_scalar(c, 0)
+        round_pair(nc.scalar.copy, 0, 0, S)
         gather_and_add(2, 0, S)
-        for c in range(LAST):
-            gather_and_add(3, c * PIECE, PIECE)
-            round_pair_on_scalar(c, 2)
+        for first, count in ((0, 192), (192, 256), (448, 64)):
+            gather_and_add(3, first, count)
+        round_pair(nc.scalar.copy, 2, 0, 128)
+        round_pair(nc.scalar.copy, 2, 128, 192)
+        round_pair(nc.scalar.copy, 2, 192, 258)
+        round_pair(nc.vector.tensor_copy, 2, 258, 384)
+        round_pair(nc.scalar.copy, 2, 384, 448)
+        round_pair(nc.scalar.copy, 2, 448, 512)
 
         res_sb = sb.tile([P, S], F32, name="res_sb")
 
-        def round_last_chunk_on_vector():
-            tile = sb.tile([P, CHUNKS[LAST], PACK], BF16, name="h_bf_last", tag="h_bf0", align_bytes=64)
-            nc.vector.tensor_copy(
-                tile[:].rearrange("p (g i) t -> p g t i", i=LINE),
-                h[:, :, STARTS[LAST] : S].rearrange("p t (g i) -> p g t i", i=LINE),
-            )
-            h_bf.append(tile)
-
         def second_product(c):
             n = CHUNKS[c]
-            h_codes = sb.tile([P, n], U32, name="h_codes%d" % c, tag="h_codes%d" % (c % LAST), align_bytes=64)
+            h_codes = sb.tile([P, n], U32, name="h_codes%d" % c, align_bytes=64)
             h_sc = sb.tile([P, n], U8, name="h_sc%d" % c, align_bytes=64)
-            nc.vector.quantize_mx(out=h_codes[:].bitcast(FP8X4), scales=h_sc[:], in_=h_bf[c][:].rearrange("p n t -> p (n t)"))
+            nc.vector.quantize_mx(out=h_codes[:].bitcast(FP8X4), scales=h_sc[:], in_=h_bf[:, STARTS[c] : STARTS[c + 1], :].rearrange("p n t -> p (n t)"))
             res = ps.tile([P, n], F32, name="res%d" % c, tag="bank%d" % c)
             nc.tensor.matmul_mx(
                 out=res[:],
@@ -155,7 +150,6 @@ def tile_picked_posadd_none_l_kernel(tc, xT, w1, w2_words, w2_scales, pe, offs, 
         second_product(0)
         second_product(1)
         store(nc.sync, 0, 1)
-        round_last_chunk_on_vector()
         second_product(2)
         store(nc.scalar, 2, 2)
         second_product(3)

@@ -17,11 +17,11 @@ ADD = mybir.AluOpType.add
 P = 128
 PACK = 4
 HALF = S // 2
-PIECE = 128
-CHUNKS = (128, 128, 128, 64, 64)
+CHUNKS = (128, 64, 128, 128, 64)
 STARTS = tuple(sum(CHUNKS[:c]) for c in range(len(CHUNKS) + 1))
-LAST = len(CHUNKS) - 1
-FIRST_ON_VECTOR = 3
+PIECES = ((0, 1), (2, 3), (4, 4))
+ROUNDED_ON_VECTOR = 2
+FIRST_COPIED_ON_VECTOR = 3
 
 
 def tile_picked_posadd_none_l_kernel(tc, xT, w1, w2_words, w2_scales, pe, offs, out):
@@ -75,10 +75,7 @@ def tile_picked_posadd_none_l_kernel(tc, xT, w1, w2_words, w2_scales, pe, offs, 
             w1_sc.append(sb.tile([P, 2 * P], U8, name="w1_sc%d" % u, align_bytes=64))
             nc.vector.quantize_mx(out=w1_codes[u][:].bitcast(FP8X4), scales=w1_sc[u][:], in_=w1_bf[:])
 
-        prod = [None] + [sb.tile([P, S], F32, name="prod%d" % t) for t in range(1, PACK)]
-        h = sb.tile([P, PACK, S], F32, name="h", tag="w1_bf1", align_bytes=64)
-        picked0 = sb.tile([P, S], F32, name="picked0", tag="w1_bf0", align_bytes=64)
-        nc.vector.tensor_copy(picked0[:], pe_plane[0][:].indirect(offsets[:]))
+        prod = [sb.tile([P, S], F32, name="prod%d" % t) for t in range(PACK)]
         for t in (0, 1, 3, 2):
             u, e = divmod(t, 2)
             w1_cols = slice(e * P, (e + 1) * P)
@@ -93,41 +90,35 @@ def tile_picked_posadd_none_l_kernel(tc, xT, w1, w2_words, w2_scales, pe, offs, 
                     start=True,
                     stop=True,
                 )
-                cols = slice(a * HALF, (a + 1) * HALF)
-                if t == 0:
-                    nc.vector.tensor_tensor(h[:, 0, cols], picked0[:, cols], acc[:], ADD)
-                else:
-                    nc.scalar.copy(out=prod[t][:, cols], in_=acc[:])
+                nc.scalar.copy(out=prod[t][:, a * HALF : (a + 1) * HALF], in_=acc[:])
 
+        h = sb.tile([P, PACK, S], F32, name="h")
         h_bf = sb.tile([P, S, PACK], BF16, name="h_bf", align_bytes=64)
+
+        def gather_and_add(t, first, stop):
+            picked = pe_plane[t][:].indirect(offsets[:, first // 16 : stop // 16])
+            nc.vector.tensor_tensor(h[:, t, first:stop], picked, prod[t][:, first:stop], ADD)
 
         def round_pair(copy, t, first, stop):
             copy(h_bf[:, first:stop, t : t + 2], h[:, t : t + 2, first:stop].rearrange("p e n -> p n e"))
 
-        def gather_and_add(t, first, count):
-            piece = slice(first, first + count)
-            picked = pe_plane[t][:].indirect(offsets[:, first // 16 : (first + count) // 16])
-            nc.vector.tensor_tensor(h[:, t, piece], picked, prod[t][:, piece], ADD)
-
+        gather_and_add(0, 0, S)
         gather_and_add(1, 0, S)
         round_pair(nc.scalar.copy, 0, 0, S)
         gather_and_add(2, 0, S)
-        for first, count in ((0, 192), (192, 256), (448, 64)):
-            gather_and_add(3, first, count)
-        round_pair(nc.scalar.copy, 2, 0, 128)
-        round_pair(nc.scalar.copy, 2, 128, 192)
-        round_pair(nc.scalar.copy, 2, 192, 258)
-        round_pair(nc.vector.tensor_copy, 2, 258, 384)
-        round_pair(nc.scalar.copy, 2, 384, 448)
-        round_pair(nc.scalar.copy, 2, 448, 512)
+        for first_chunk, last_chunk in PIECES:
+            gather_and_add(3, STARTS[first_chunk], STARTS[last_chunk + 1])
+        for c in range(len(CHUNKS)):
+            round_pair(nc.vector.tensor_copy if c == ROUNDED_ON_VECTOR else nc.scalar.copy, 2, STARTS[c], STARTS[c + 1])
 
         res_sb = sb.tile([P, S], F32, name="res_sb")
 
         def second_product(c):
             n = CHUNKS[c]
+            chunk = slice(STARTS[c], STARTS[c + 1])
             h_codes = sb.tile([P, n], U32, name="h_codes%d" % c, align_bytes=64)
             h_sc = sb.tile([P, n], U8, name="h_sc%d" % c, align_bytes=64)
-            nc.vector.quantize_mx(out=h_codes[:].bitcast(FP8X4), scales=h_sc[:], in_=h_bf[:, STARTS[c] : STARTS[c + 1], :].rearrange("p n t -> p (n t)"))
+            nc.vector.quantize_mx(out=h_codes[:].bitcast(FP8X4), scales=h_sc[:], in_=h_bf[:, chunk, :].rearrange("p n t -> p (n t)"))
             res = ps.tile([P, n], F32, name="res%d" % c, tag="bank%d" % c)
             nc.tensor.matmul_mx(
                 out=res[:],
@@ -138,10 +129,10 @@ def tile_picked_posadd_none_l_kernel(tc, xT, w1, w2_words, w2_scales, pe, offs, 
                 start=True,
                 stop=True,
             )
-            if c >= FIRST_ON_VECTOR:
-                nc.vector.tensor_copy(res_sb[:, STARTS[c] : STARTS[c + 1]], res[:])
+            if c >= FIRST_COPIED_ON_VECTOR:
+                nc.vector.tensor_copy(res_sb[:, chunk], res[:])
             else:
-                nc.scalar.copy(out=res_sb[:, STARTS[c] : STARTS[c + 1]], in_=res[:])
+                nc.scalar.copy(out=res_sb[:, chunk], in_=res[:])
 
         def store(queue, first_chunk, last_chunk):
             out_cols = slice(STARTS[first_chunk], STARTS[last_chunk + 1])
@@ -153,5 +144,5 @@ def tile_picked_posadd_none_l_kernel(tc, xT, w1, w2_words, w2_scales, pe, offs, 
         second_product(2)
         store(nc.scalar, 2, 2)
         second_product(3)
-        second_product(LAST)
-        store(nc.sync, FIRST_ON_VECTOR, LAST)
+        second_product(4)
+        store(nc.sync, 3, 4)

@@ -33,10 +33,8 @@ def tile_picked_posadd_none_l_kernel(tc, xT, w1, w2_words, w2_scales, pe, offs, 
         offsets = sb.tile([P, S // 16], U16, name="offsets")
         w1_raw = sb.tile([P, PACK, H], F32, name="w1_raw")
 
-        w2_codes = sb.tile([P, N], U32, name="w2_codes", align_bytes=64)
         w2_sc = sb.tile([P, N], U8, name="w2_sc", align_bytes=64)
         nc.vector.memset(w2_sc[:].bitcast(I32), 0)
-        nc.scalar.dma_start(w2_codes[:].bitcast(I32), w2_words[0].rearrange("p n t -> p (n t)").bitcast(I32))
         for q in range(4):
             nc.scalar.dma_start(w2_sc[32 * q : 32 * q + 4, :].bitcast(I32), w2_scales[0, 4 * q : 4 * q + 4, :].bitcast(I32))
 
@@ -75,7 +73,7 @@ def tile_picked_posadd_none_l_kernel(tc, xT, w1, w2_words, w2_scales, pe, offs, 
             w1_sc.append(sb.tile([P, 2 * P], U8, name="w1_sc%d" % u, align_bytes=64))
             nc.vector.quantize_mx(out=w1_codes[u][:].bitcast(FP8X4), scales=w1_sc[u][:], in_=w1_bf[:])
 
-        prod = [sb.tile([P, S], F32, name="prod%d" % t) for t in range(PACK)]
+        prod = [sb.tile([P, S], F32, name="prod%d" % t, tag="prod%d" % t, align_bytes=64) for t in range(PACK)]
         for t in (0, 1, 3, 2):
             u, e = divmod(t, 2)
             w1_cols = slice(e * P, (e + 1) * P)
@@ -106,6 +104,8 @@ def tile_picked_posadd_none_l_kernel(tc, xT, w1, w2_words, w2_scales, pe, offs, 
         gather_and_add(1, 0, S)
         round_pair(nc.scalar.copy, 0, 0, S)
         gather_and_add(2, 0, S)
+        w2_codes = sb.tile([P, N], U32, name="w2_codes", tag="prod2", align_bytes=64)
+        nc.sync.dma_start(w2_codes[:].bitcast(I32), w2_words[0].rearrange("p n t -> p (n t)").bitcast(I32))
         for first_chunk, last_chunk in PIECES:
             gather_and_add(3, STARTS[first_chunk], STARTS[last_chunk + 1])
         for c in range(len(CHUNKS)):

@@ -142,7 +142,7 @@ def tile_picked_posadd_none_l_kernel(tc, xT, w1, w2_words, w2_scales, pe, offs, 
         second_product(1)
         store(nc.sync, 0, 1)
         second_product(2)
-        store(nc.scalar, 2, 2)
+        store(nc.sync, 2, 2)
         second_product(3)
         second_product(4)
         store(nc.sync, 3, 4)

@@ -33,17 +33,16 @@ def tile_picked_posadd_none_l_kernel(tc, xT, w1, w2_words, w2_scales, pe, offs, 
         offsets = sb.tile([P, S // 16], U16, name="offsets")
         w1_raw = sb.tile([P, PACK, H], F32, name="w1_raw")
 
-        w2_sc = sb.tile([P, N], U8, name="w2_sc", align_bytes=64)
-        nc.vector.memset(w2_sc[:].bitcast(I32), 0)
-        for q in range(4):
-            nc.scalar.dma_start(w2_sc[32 * q : 32 * q + 4, :].bitcast(I32), w2_scales[0, 4 * q : 4 * q + 4, :].bitcast(I32))
-
         x_rows = xT.rearrange("(p u e) t -> u p e t", u=2, e=2)
         pe_rows = pe.rearrange("(p t) c -> t p c", t=PACK)
         x_pair = [sb.tile([P, 2, T], F32, name="x_pair%d" % u) for u in range(2)]
         pe_plane = [sb.tile([P, T], F32, name="pe_plane%d" % t) for t in range(PACK)]
         nc.sync.dma_start(x_pair[0][:], x_rows[0])
         nc.sync.dma_start(offsets[:], offs)
+        w2_sc = sb.tile([P, N], U8, name="w2_sc", align_bytes=64)
+        nc.vector.memset(w2_sc[:].bitcast(I32), 0)
+        for q in range(4):
+            nc.sync.dma_start(w2_sc[32 * q : 32 * q + 4, :].bitcast(I32), w2_scales[0, 4 * q : 4 * q + 4, :].bitcast(I32))
         nc.sync.dma_start(x_pair[1][:], x_rows[1])
         nc.sync.dma_start(w1_raw[:], w1.rearrange("(p j) c -> p j c", j=PACK))
         for t in range(PACK):

@@ -20,8 +20,9 @@ HALF = S // 2
 CHUNKS = (128, 64, 128, 128, 64)
 STARTS = tuple(sum(CHUNKS[:c]) for c in range(len(CHUNKS) + 1))
 PIECES = ((0, 1), (2, 3), (4, 4))
-ROUNDED_ON_VECTOR = 2
+ROUNDED_ON_VECTOR = (2,)
 FIRST_COPIED_ON_VECTOR = 3
+STORES = ((0, 1), (2, 2), (3, 4))
 
 
 def tile_picked_posadd_none_l_kernel(tc, xT, w1, w2_words, w2_scales, pe, offs, out):
@@ -32,17 +33,21 @@ def tile_picked_posadd_none_l_kernel(tc, xT, w1, w2_words, w2_scales, pe, offs, 
 
         offsets = sb.tile([P, S // 16], U16, name="offsets")
         w1_raw = sb.tile([P, PACK, H], F32, name="w1_raw")
+        w2_sc = sb.tile([P, N], U8, name="w2_sc", align_bytes=64)
+        nc.vector.memset(w2_sc[:].bitcast(I32), 0)
 
         x_rows = xT.rearrange("(p u e) t -> u p e t", u=2, e=2)
         pe_rows = pe.rearrange("(p t) c -> t p c", t=PACK)
         x_pair = [sb.tile([P, 2, T], F32, name="x_pair%d" % u) for u in range(2)]
         pe_plane = [sb.tile([P, T], F32, name="pe_plane%d" % t) for t in range(PACK)]
+
+        def load_scales():
+            for q in range(4):
+                nc.sync.dma_start(w2_sc[32 * q : 32 * q + 4, :].bitcast(I32), w2_scales[0, 4 * q : 4 * q + 4, :].bitcast(I32))
+
         nc.sync.dma_start(x_pair[0][:], x_rows[0])
         nc.sync.dma_start(offsets[:], offs)
-        w2_sc = sb.tile([P, N], U8, name="w2_sc", align_bytes=64)
-        nc.vector.memset(w2_sc[:].bitcast(I32), 0)
-        for q in range(4):
-            nc.sync.dma_start(w2_sc[32 * q : 32 * q + 4, :].bitcast(I32), w2_scales[0, 4 * q : 4 * q + 4, :].bitcast(I32))
+        load_scales()
         nc.sync.dma_start(x_pair[1][:], x_rows[1])
         nc.sync.dma_start(w1_raw[:], w1.rearrange("(p j) c -> p j c", j=PACK))
         for t in range(PACK):
@@ -96,19 +101,23 @@ def tile_picked_posadd_none_l_kernel(tc, xT, w1, w2_words, w2_scales, pe, offs, 
             picked = pe_plane[t][:].indirect(offsets[:, first // 16 : stop // 16])
             nc.vector.tensor_tensor(h[:, t, first:stop], picked, prod[t][:, first:stop], ADD)
 
-        def round_pair(copy, t, first, stop):
-            copy(h_bf[:, first:stop, t : t + 2], h[:, t : t + 2, first:stop].rearrange("p e n -> p n e"))
+        def round_plane(copy, t, first, stop):
+            copy(h_bf[:, first:stop, t], h[:, t, first:stop])
 
         gather_and_add(0, 0, S)
         gather_and_add(1, 0, S)
-        round_pair(nc.scalar.copy, 0, 0, S)
-        gather_and_add(2, 0, S)
+        nc.scalar.copy(h_bf[:, :, 0:2], h[:, 0:2, :].rearrange("p e n -> p n e"))
+        gather_and_add(2, 0, HALF)
+        gather_and_add(2, HALF, S)
         w2_codes = sb.tile([P, N], U32, name="w2_codes", tag="prod2", align_bytes=64)
         nc.sync.dma_start(w2_codes[:].bitcast(I32), w2_words[0].rearrange("p n t -> p (n t)").bitcast(I32))
+        round_plane(nc.scalar.copy, 2, 0, STARTS[2])
+        round_plane(nc.scalar.copy, 2, STARTS[3], S)
+        round_plane(nc.vector.tensor_copy, 2, STARTS[2], STARTS[3])
         for first_chunk, last_chunk in PIECES:
             gather_and_add(3, STARTS[first_chunk], STARTS[last_chunk + 1])
         for c in range(len(CHUNKS)):
-            round_pair(nc.vector.tensor_copy if c == ROUNDED_ON_VECTOR else nc.scalar.copy, 2, STARTS[c], STARTS[c + 1])
+            round_plane(nc.vector.tensor_copy if c in ROUNDED_ON_VECTOR else nc.scalar.copy, 3, STARTS[c], STARTS[c + 1])
 
         res_sb = sb.tile([P, S], F32, name="res_sb")
 
@@ -133,15 +142,8 @@ def tile_picked_posadd_none_l_kernel(tc, xT, w1, w2_words, w2_scales, pe, offs, 
             else:
                 nc.scalar.copy(out=res_sb[:, chunk], in_=res[:])
 
-        def store(queue, first_chunk, last_chunk):
+        for first_chunk, last_chunk in STORES:
+            for c in range(first_chunk, last_chunk + 1):
+                second_product(c)
             out_cols = slice(STARTS[first_chunk], STARTS[last_chunk + 1])
-            queue.dma_start(out[:, out_cols], res_sb[:, out_cols])
-
-        second_product(0)
-        second_product(1)
-        store(nc.sync, 0, 1)
-        second_product(2)
-        store(nc.sync, 2, 2)
-        second_product(3)
-        second_product(4)
-        store(nc.sync, 3, 4)
+            nc.sync.dma_start(out[:, out_cols], res_sb[:, out_cols])

@@ -106,18 +106,22 @@ def tile_picked_posadd_none_l_kernel(tc, xT, w1, w2_words, w2_scales, pe, offs, 
 
         gather_and_add(0, 0, S)
         gather_and_add(1, 0, S)
-        nc.scalar.copy(h_bf[:, :, 0:2], h[:, 0:2, :].rearrange("p e n -> p n e"))
+        nc.scalar.copy(h_bf[:, :HALF, 0:2], h[:, 0:2, :HALF].rearrange("p e n -> p n e"))
+        nc.vector.tensor_copy(h_bf[:, HALF:, 0:2], h[:, 0:2, HALF:].rearrange("p e n -> p n e"))
         gather_and_add(2, 0, HALF)
         gather_and_add(2, HALF, S)
         w2_codes = sb.tile([P, N], U32, name="w2_codes", tag="prod2", align_bytes=64)
         nc.sync.dma_start(w2_codes[:].bitcast(I32), w2_words[0].rearrange("p n t -> p (n t)").bitcast(I32))
         round_plane(nc.scalar.copy, 2, 0, STARTS[2])
         round_plane(nc.scalar.copy, 2, STARTS[3], S)
-        round_plane(nc.vector.tensor_copy, 2, STARTS[2], STARTS[3])
         for first_chunk, last_chunk in PIECES:
             gather_and_add(3, STARTS[first_chunk], STARTS[last_chunk + 1])
         for c in range(len(CHUNKS)):
-            round_plane(nc.vector.tensor_copy if c in ROUNDED_ON_VECTOR else nc.scalar.copy, 3, STARTS[c], STARTS[c + 1])
+            if c in ROUNDED_ON_VECTOR:
+                chunk = slice(STARTS[c], STARTS[c + 1])
+                nc.vector.tensor_copy(h_bf[:, chunk, 2:4], h[:, 2:4, chunk].rearrange("p e n -> p n e"))
+            else:
+                round_plane(nc.scalar.copy, 3, STARTS[c], STARTS[c + 1])
 
         res_sb = sb.tile([P, S], F32, name="res_sb")
 

@@ -13,16 +13,11 @@ U16 = mybir.dt.uint16
 U8 = mybir.dt.uint8
 FP8X4 = mybir.dt.float8_e4m3fn_x4
 ADD = mybir.AluOpType.add
+COPY = mybir.ActivationFunctionType.Copy
 
 P = 128
 PACK = 4
 HALF = S // 2
-CHUNKS = (128, 64, 128, 128, 64)
-STARTS = tuple(sum(CHUNKS[:c]) for c in range(len(CHUNKS) + 1))
-PIECES = ((0, 1), (2, 3), (4, 4))
-ROUNDED_ON_VECTOR = (2,)
-FIRST_COPIED_ON_VECTOR = 3
-STORES = ((0, 1), (2, 2), (3, 4))
 
 
 def tile_picked_posadd_none_l_kernel(tc, xT, w1, w2_words, w2_scales, pe, offs, out):
@@ -36,35 +31,32 @@ def tile_picked_posadd_none_l_kernel(tc, xT, w1, w2_words, w2_scales, pe, offs, 
         w2_sc = sb.tile([P, N], U8, name="w2_sc", align_bytes=64)
         nc.vector.memset(w2_sc[:].bitcast(I32), 0)
 
-        x_rows = xT.rearrange("(p u e) t -> u p e t", u=2, e=2)
-        pe_rows = pe.rearrange("(p t) c -> t p c", t=PACK)
+        x_rows = xT.rearrange("(p u e) c -> u p e c", u=2, e=2)
         x_pair = [sb.tile([P, 2, T], F32, name="x_pair%d" % u) for u in range(2)]
-        pe_plane = [sb.tile([P, T], F32, name="pe_plane%d" % t) for t in range(PACK)]
+        pe_rows = pe.rearrange("(p t) c -> p t c", t=PACK)
+        pe_first = [sb.tile([P, T], F32, name="pe_first%d" % t, tag="pe_first%d" % t) for t in range(2)]
+        pe_third = sb.tile([P, T], F32, name="pe_third")
+        pe_last = sb.tile([P, T], F32, name="pe_last")
 
-        def load_scales():
-            for q in range(4):
-                nc.sync.dma_start(w2_sc[32 * q : 32 * q + 4, :].bitcast(I32), w2_scales[0, 4 * q : 4 * q + 4, :].bitcast(I32))
-
-        nc.sync.dma_start(x_pair[0][:], x_rows[0])
-        nc.sync.dma_start(offsets[:], offs)
-        load_scales()
-        nc.sync.dma_start(x_pair[1][:], x_rows[1])
         nc.sync.dma_start(w1_raw[:], w1.rearrange("(p j) c -> p j c", j=PACK))
-        for t in range(PACK):
-            nc.sync.dma_start(pe_plane[t][:], pe_rows[t])
-
-        x_bf = sb.tile([P, S, PACK], BF16, name="x_bf", align_bytes=64)
+        nc.sync.dma_start(offsets[:], offs)
+        for q in range(4):
+            nc.sync.dma_start(w2_sc[32 * q : 32 * q + 4, :].bitcast(I32), w2_scales[0, 4 * q : 4 * q + 4, :].bitcast(I32))
         for u in range(2):
-            for e in range(2):
-                nc.vector.tensor_copy(x_bf[:, :, 2 * u + e], x_pair[u][:, e, :].indirect(offsets[:]))
-        x_codes = [sb.tile([P, HALF], U32, name="x_codes%d" % a, align_bytes=64) for a in range(2)]
-        x_sc = [sb.tile([P, HALF], U8, name="x_sc%d" % a, align_bytes=64) for a in range(2)]
-        for a in range(2):
-            nc.vector.quantize_mx(
-                out=x_codes[a][:].bitcast(FP8X4),
-                scales=x_sc[a][:],
-                in_=x_bf[:, a * HALF : (a + 1) * HALF, :].rearrange("p n j -> p (n j)"),
-            )
+            nc.sync.dma_start(x_pair[u][:], x_rows[u])
+        for t in range(2):
+            nc.sync.dma_start(pe_first[t][:], pe_rows[:, t, :])
+        nc.sync.dma_start(pe_third[:], pe_rows[:, 2, :])
+        nc.sync.dma_start(pe_last[:], pe_rows[:, 3, :])
+
+        def entries(first, stop):
+            return offsets[:, first // 16 : stop // 16]
+
+        def gather_on_vector(dst, window, first, stop):
+            nc.vector.tensor_copy(dst, window.indirect(entries(first, stop)))
+
+        def gather_on_scalar(dst, window, first, stop):
+            nc.scalar.activation(dst, window.indirect(entries(first, stop)), COPY)
 
         w1_codes, w1_sc = [], []
         for u in range(2):
@@ -77,61 +69,79 @@ def tile_picked_posadd_none_l_kernel(tc, xT, w1, w2_words, w2_scales, pe, offs, 
             w1_sc.append(sb.tile([P, 2 * P], U8, name="w1_sc%d" % u, align_bytes=64))
             nc.vector.quantize_mx(out=w1_codes[u][:].bitcast(FP8X4), scales=w1_sc[u][:], in_=w1_bf[:])
 
-        prod = [sb.tile([P, S], F32, name="prod%d" % t, tag="prod%d" % t, align_bytes=64) for t in range(PACK)]
-        for t in (0, 1, 3, 2):
-            u, e = divmod(t, 2)
-            w1_cols = slice(e * P, (e + 1) * P)
-            for a in range(2):
-                acc = ps.tile([P, HALF], F32, name="acc%d%d" % (t, a), tag="bank%d" % (2 * t + a))
-                nc.tensor.matmul_mx(
-                    out=acc[:],
-                    lhsT=w1_codes[u][:, w1_cols].bitcast(FP8X4),
-                    lhsT_scale=w1_sc[u][:, w1_cols],
-                    rhs=x_codes[a][:].bitcast(FP8X4),
-                    rhs_scale=x_sc[a][:],
-                    start=True,
-                    stop=True,
-                )
-                nc.scalar.copy(out=prod[t][:, a * HALF : (a + 1) * HALF], in_=acc[:])
+        acc = [ps.tile([P, S], F32, name="acc%d" % t, tag="bank%d" % t) for t in range(PACK)]
+        x_bf = sb.tile([P, S, PACK], BF16, name="x_bf", align_bytes=64)
+        x_picked = [sb.tile([P, 2, S], F32, name="x_picked%d" % u) for u in range(2)]
 
+        def pick_x(u, first, stop):
+            gather_on_vector(x_picked[u][:, 0, first:stop], x_pair[u][:, 0, :], first, stop)
+            gather_on_scalar(x_picked[u][:, 1, first:stop], x_pair[u][:, 1, :], first, stop)
+
+        def round_x(u, first, stop):
+            nc.vector.tensor_copy(x_bf[:, first:stop, 2 * u : 2 * u + 2], x_picked[u][:, :, first:stop].rearrange("p e n -> p n e"))
+
+        pick_x(0, 0, S)
+        round_x(0, 0, S)
+        pick_x(1, 0, HALF)
+        pick_x(1, HALF, S)
+        round_x(1, 0, HALF)
+        round_x(1, HALF, S)
+        x_codes = [sb.tile([P, HALF], U32, name="x_codes%d" % a, align_bytes=64) for a in range(2)]
+        x_sc = [sb.tile([P, HALF], U8, name="x_sc%d" % a, align_bytes=64) for a in range(2)]
+        for a in range(2):
+            nc.vector.quantize_mx(
+                out=x_codes[a][:].bitcast(FP8X4),
+                scales=x_sc[a][:],
+                in_=x_bf[:, a * HALF : (a + 1) * HALF, :].rearrange("p n j -> p (n j)"),
+            )
+        for u in range(2):
+            for a in range(2):
+                for e in range(2):
+                    w1_cols = slice(e * P, (e + 1) * P)
+                    nc.tensor.matmul_mx(
+                        out=acc[2 * u + e][:, a * HALF : (a + 1) * HALF],
+                        lhsT=w1_codes[u][:, w1_cols].bitcast(FP8X4),
+                        lhsT_scale=w1_sc[u][:, w1_cols],
+                        rhs=x_codes[a][:].bitcast(FP8X4),
+                        rhs_scale=x_sc[a][:],
+                        start=True,
+                        stop=True,
+                    )
+
+        picked = {t: sb.tile([P, S], F32, name="picked%d" % t, tag="picked%d" % t, align_bytes=64) for t in (0, 1, 3)}
         h = sb.tile([P, PACK, S], F32, name="h")
         h_bf = sb.tile([P, S, PACK], BF16, name="h_bf", align_bytes=64)
 
-        def gather_and_add(t, first, stop):
-            picked = pe_plane[t][:].indirect(offsets[:, first // 16 : stop // 16])
-            nc.vector.tensor_tensor(h[:, t, first:stop], picked, prod[t][:, first:stop], ADD)
+        def add(t, first, stop):
+            nc.vector.tensor_tensor(h[:, t, first:stop], acc[t][:, first:stop], picked[t][:, first:stop], ADD)
 
-        def round_plane(copy, t, first, stop):
-            copy(h_bf[:, first:stop, t], h[:, t, first:stop])
+        def round_pair(copy, u, first, stop):
+            copy(h_bf[:, first:stop, 2 * u : 2 * u + 2], h[:, 2 * u : 2 * u + 2, first:stop].rearrange("p e n -> p n e"))
 
-        gather_and_add(0, 0, S)
-        gather_and_add(1, 0, S)
-        nc.scalar.copy(h_bf[:, :HALF, 0:2], h[:, 0:2, :HALF].rearrange("p e n -> p n e"))
-        nc.vector.tensor_copy(h_bf[:, HALF:, 0:2], h[:, 0:2, HALF:].rearrange("p e n -> p n e"))
-        gather_and_add(2, 0, HALF)
-        gather_and_add(2, HALF, S)
-        w2_codes = sb.tile([P, N], U32, name="w2_codes", tag="prod2", align_bytes=64)
+        gather_on_scalar(picked[0][:], pe_first[0][:], 0, S)
+        prod_late = sb.tile([P, 2, S], F32, name="prod_late", tag="pe_first0")
+        prod_third, prod_last = prod_late[:, 0, :], prod_late[:, 1, :]
+        nc.scalar.copy(out=prod_third, in_=acc[2][:])
+        nc.scalar.copy(out=prod_last.rearrange("p (a n) -> p a n", n=128)[:, 0:3:2, :], in_=acc[3][:].rearrange("p (a n) -> p a n", n=128)[:, 0:3:2, :])
+        add(0, 0, S)
+        gather_on_vector(picked[1][:, :HALF], pe_first[1][:], 0, HALF)
+        gather_on_vector(picked[1][:, HALF:], pe_first[1][:], HALF, S)
+        add(1, 0, HALF)
+        add(1, HALF, S)
+        round_pair(nc.scalar.copy, 0, 0, HALF)
+        round_pair(nc.scalar.copy, 0, HALF, S)
+        nc.vector.tensor_tensor(h[:, 2, :], pe_third[:].indirect(offsets[:]), prod_third, ADD)
+        w2_codes = sb.tile([P, N], U32, name="w2_codes", tag="picked1", align_bytes=64)
         nc.sync.dma_start(w2_codes[:].bitcast(I32), w2_words[0].rearrange("p n t -> p (n t)").bitcast(I32))
-        round_plane(nc.scalar.copy, 2, 0, STARTS[2])
-        round_plane(nc.scalar.copy, 2, STARTS[3], S)
-        for first_chunk, last_chunk in PIECES:
-            gather_and_add(3, STARTS[first_chunk], STARTS[last_chunk + 1])
-        for c in range(len(CHUNKS)):
-            if c in ROUNDED_ON_VECTOR:
-                chunk = slice(STARTS[c], STARTS[c + 1])
-                nc.vector.tensor_copy(h_bf[:, chunk, 2:4], h[:, 2:4, chunk].rearrange("p e n -> p n e"))
-            else:
-                round_plane(nc.scalar.copy, 3, STARTS[c], STARTS[c + 1])
 
         res_sb = sb.tile([P, S], F32, name="res_sb")
 
-        def second_product(c):
-            n = CHUNKS[c]
-            chunk = slice(STARTS[c], STARTS[c + 1])
+        def second_product(c, first, stop, copy):
+            n = stop - first
             h_codes = sb.tile([P, n], U32, name="h_codes%d" % c, align_bytes=64)
             h_sc = sb.tile([P, n], U8, name="h_sc%d" % c, align_bytes=64)
-            nc.vector.quantize_mx(out=h_codes[:].bitcast(FP8X4), scales=h_sc[:], in_=h_bf[:, chunk, :].rearrange("p n t -> p (n t)"))
-            res = ps.tile([P, n], F32, name="res%d" % c, tag="bank%d" % c)
+            nc.vector.quantize_mx(out=h_codes[:].bitcast(FP8X4), scales=h_sc[:], in_=h_bf[:, first:stop, :].rearrange("p n t -> p (n t)"))
+            res = ps.tile([P, n], F32, name="res%d" % c, tag="bank%d" % ((4 + c) % 8))
             nc.tensor.matmul_mx(
                 out=res[:],
                 lhsT=w2_codes[:].bitcast(FP8X4),
@@ -141,13 +151,30 @@ def tile_picked_posadd_none_l_kernel(tc, xT, w1, w2_words, w2_scales, pe, offs, 
                 start=True,
                 stop=True,
             )
-            if c >= FIRST_COPIED_ON_VECTOR:
-                nc.vector.tensor_copy(res_sb[:, chunk], res[:])
-            else:
-                nc.scalar.copy(out=res_sb[:, chunk], in_=res[:])
+            copy(res_sb[:, first:stop], res[:])
 
-        for first_chunk, last_chunk in STORES:
-            for c in range(first_chunk, last_chunk + 1):
-                second_product(c)
-            out_cols = slice(STARTS[first_chunk], STARTS[last_chunk + 1])
-            nc.sync.dma_start(out[:, out_cols], res_sb[:, out_cols])
+        def store(first, stop):
+            nc.sync.dma_start(out[:, first:stop], res_sb[:, first:stop])
+
+        def fused(first, stop):
+            nc.vector.tensor_tensor(h[:, 3, first:stop], pe_last[:].indirect(entries(first, stop)), prod_last[:, first:stop], ADD)
+
+        gather_on_scalar(picked[3][:, 128:256], pe_last[:], 128, 256)
+        gather_on_scalar(picked[3][:, 384:512], pe_last[:], 384, 512)
+        fused(0, 128)
+        fused(256, 384)
+        add(3, 128, 256)
+        add(3, 384, 512)
+        round_pair(nc.scalar.copy, 1, 0, 128)
+        round_pair(nc.scalar.copy, 1, 256, 384)
+        round_pair(nc.scalar.copy, 1, 448, 512)
+        round_pair(nc.vector.tensor_copy, 1, 128, 256)
+        second_product(0, 0, 128, nc.scalar.copy)
+        round_pair(nc.vector.tensor_copy, 1, 384, 448)
+        second_product(1, 128, 256, nc.scalar.copy)
+        store(0, 256)
+        second_product(2, 256, 384, nc.scalar.copy)
+        store(256, 384)
+        second_product(3, 384, 448, nc.vector.tensor_copy)
+        second_product(4, 448, 512, nc.vector.tensor_copy)
+        store(384, 512)

@@ -34,7 +34,7 @@ def tile_picked_posadd_none_l_kernel(tc, xT, w1, w2_words, w2_scales, pe, offs, 
         x_rows = xT.rearrange("(p u e) c -> u p e c", u=2, e=2)
         x_pair = [sb.tile([P, 2, T], F32, name="x_pair%d" % u) for u in range(2)]
         pe_rows = pe.rearrange("(p t) c -> p t c", t=PACK)
-        pe_first = [sb.tile([P, T], F32, name="pe_first%d" % t, tag="pe_first%d" % t) for t in range(2)]
+        pe_first = sb.tile([P, 2, T], F32, name="pe_first")
         pe_third = sb.tile([P, T], F32, name="pe_third")
         pe_last = sb.tile([P, T], F32, name="pe_last")
 
@@ -44,8 +44,7 @@ def tile_picked_posadd_none_l_kernel(tc, xT, w1, w2_words, w2_scales, pe, offs, 
             nc.sync.dma_start(w2_sc[32 * q : 32 * q + 4, :].bitcast(I32), w2_scales[0, 4 * q : 4 * q + 4, :].bitcast(I32))
         for u in range(2):
             nc.sync.dma_start(x_pair[u][:], x_rows[u])
-        for t in range(2):
-            nc.sync.dma_start(pe_first[t][:], pe_rows[:, t, :])
+        nc.sync.dma_start(pe_first[:], pe_rows[:, 0:2, :])
         nc.sync.dma_start(pe_third[:], pe_rows[:, 2, :])
         nc.sync.dma_start(pe_last[:], pe_rows[:, 3, :])
 
@@ -94,7 +93,7 @@ def tile_picked_posadd_none_l_kernel(tc, xT, w1, w2_words, w2_scales, pe, offs, 
                 scales=x_sc[a][:],
                 in_=x_bf[:, a * HALF : (a + 1) * HALF, :].rearrange("p n j -> p (n j)"),
             )
-        for u in range(2):
+        for u in (1, 0):
             for a in range(2):
                 for e in range(2):
                     w1_cols = slice(e * P, (e + 1) * P)
@@ -118,18 +117,17 @@ def tile_picked_posadd_none_l_kernel(tc, xT, w1, w2_words, w2_scales, pe, offs, 
         def round_pair(copy, u, first, stop):
             copy(h_bf[:, first:stop, 2 * u : 2 * u + 2], h[:, 2 * u : 2 * u + 2, first:stop].rearrange("p e n -> p n e"))
 
-        gather_on_scalar(picked[0][:], pe_first[0][:], 0, S)
-        prod_late = sb.tile([P, 2, S], F32, name="prod_late", tag="pe_first0")
+        prod_late = sb.tile([P, 2, S], F32, name="prod_late")
         prod_third, prod_last = prod_late[:, 0, :], prod_late[:, 1, :]
         nc.scalar.copy(out=prod_third, in_=acc[2][:])
         nc.scalar.copy(out=prod_last.rearrange("p (a n) -> p a n", n=128)[:, 0:3:2, :], in_=acc[3][:].rearrange("p (a n) -> p a n", n=128)[:, 0:3:2, :])
-        add(0, 0, S)
-        gather_on_vector(picked[1][:, :HALF], pe_first[1][:], 0, HALF)
-        gather_on_vector(picked[1][:, HALF:], pe_first[1][:], HALF, S)
-        add(1, 0, HALF)
-        add(1, HALF, S)
-        round_pair(nc.scalar.copy, 0, 0, HALF)
-        round_pair(nc.scalar.copy, 0, HALF, S)
+        for a in range(2):
+            gather_on_scalar(picked[0][:, a * HALF : (a + 1) * HALF], pe_first[:, 0, :], a * HALF, (a + 1) * HALF)
+            gather_on_vector(picked[1][:, a * HALF : (a + 1) * HALF], pe_first[:, 1, :], a * HALF, (a + 1) * HALF)
+        for a in range(2):
+            add(1, a * HALF, (a + 1) * HALF)
+            add(0, a * HALF, (a + 1) * HALF)
+            round_pair(nc.scalar.copy, 0, a * HALF, (a + 1) * HALF)
         nc.vector.tensor_tensor(h[:, 2, :], pe_third[:].indirect(offsets[:]), prod_third, ADD)
         w2_codes = sb.tile([P, N], U32, name="w2_codes", tag="picked1", align_bytes=64)
         nc.sync.dma_start(w2_codes[:].bitcast(I32), w2_words[0].rearrange("p n t -> p (n t)").bitcast(I32))

@@ -168,9 +168,10 @@ def tile_picked_posadd_none_l_kernel(tc, xT, w1, w2_words, w2_scales, pe, offs, 
         round_pair(nc.scalar.copy, 1, 448, 512)
         round_pair(nc.vector.tensor_copy, 1, 128, 256)
         second_product(0, 0, 128, nc.scalar.copy)
+        store(0, 128)
         round_pair(nc.vector.tensor_copy, 1, 384, 448)
         second_product(1, 128, 256, nc.scalar.copy)
-        store(0, 256)
+        store(128, 256)
         second_product(2, 256, 384, nc.scalar.copy)
         store(256, 384)
         second_product(3, 384, 448, nc.vector.tensor_copy)

@@ -130,7 +130,7 @@ def tile_picked_posadd_none_l_kernel(tc, xT, w1, w2_words, w2_scales, pe, offs, 
             round_pair(nc.scalar.copy, 0, a * HALF, (a + 1) * HALF)
         nc.vector.tensor_tensor(h[:, 2, :], pe_third[:].indirect(offsets[:]), prod_third, ADD)
         w2_codes = sb.tile([P, N], U32, name="w2_codes", tag="picked1", align_bytes=64)
-        nc.sync.dma_start(w2_codes[:].bitcast(I32), w2_words[0].rearrange("p n t -> p (n t)").bitcast(I32))
+        nc.scalar.dma_start(w2_codes[:].bitcast(I32), w2_words[0].rearrange("p n t -> p (n t)").bitcast(I32))
 
         res_sb = sb.tile([P, S], F32, name="res_sb")
 
@@ -151,8 +151,8 @@ def tile_picked_posadd_none_l_kernel(tc, xT, w1, w2_words, w2_scales, pe, offs, 
             )
             copy(res_sb[:, first:stop], res[:])
 
-        def store(first, stop):
-            nc.sync.dma_start(out[:, first:stop], res_sb[:, first:stop])
+        def store(first, stop, queue=nc.sync):
+            queue.dma_start(out[:, first:stop], res_sb[:, first:stop])
 
         def fused(first, stop):
             nc.vector.tensor_tensor(h[:, 3, first:stop], pe_last[:].indirect(entries(first, stop)), prod_last[:, first:stop], ADD)
@@ -173,7 +173,7 @@ def tile_picked_posadd_none_l_kernel(tc, xT, w1, w2_words, w2_scales, pe, offs, 
         second_product(1, 128, 256, nc.scalar.copy)
         store(128, 256)
         second_product(2, 256, 384, nc.scalar.copy)
-        store(256, 384)
+        store(256, 384, nc.scalar)
         second_product(3, 384, 448, nc.vector.tensor_copy)
         second_product(4, 448, 512, nc.vector.tensor_copy)
         store(384, 512)

@@ -120,7 +120,7 @@ def tile_picked_posadd_none_l_kernel(tc, xT, w1, w2_words, w2_scales, pe, offs, 
         prod_late = sb.tile([P, 2, S], F32, name="prod_late")
         prod_third, prod_last = prod_late[:, 0, :], prod_late[:, 1, :]
         nc.scalar.copy(out=prod_third, in_=acc[2][:])
-        nc.scalar.copy(out=prod_last.rearrange("p (a n) -> p a n", n=128)[:, 0:3:2, :], in_=acc[3][:].rearrange("p (a n) -> p a n", n=128)[:, 0:3:2, :])
+        nc.scalar.copy(out=prod_last[:, :HALF], in_=acc[3][:, :HALF])
         for a in range(2):
             gather_on_scalar(picked[0][:, a * HALF : (a + 1) * HALF], pe_first[:, 0, :], a * HALF, (a + 1) * HALF)
             gather_on_vector(picked[1][:, a * HALF : (a + 1) * HALF], pe_first[:, 1, :], a * HALF, (a + 1) * HALF)
@@ -157,19 +157,20 @@ def tile_picked_posadd_none_l_kernel(tc, xT, w1, w2_words, w2_scales, pe, offs, 
         def fused(first, stop):
             nc.vector.tensor_tensor(h[:, 3, first:stop], pe_last[:].indirect(entries(first, stop)), prod_last[:, first:stop], ADD)
 
-        gather_on_scalar(picked[3][:, 128:256], pe_last[:], 128, 256)
+        gather_on_scalar(picked[3][:, 256:384], pe_last[:], 256, 384)
         gather_on_scalar(picked[3][:, 384:512], pe_last[:], 384, 512)
         fused(0, 128)
-        fused(256, 384)
-        add(3, 128, 256)
+        fused(128, 256)
+        add(3, 256, 384)
+        round_pair(nc.vector.tensor_copy, 1, 0, 64)
         add(3, 384, 512)
-        round_pair(nc.scalar.copy, 1, 0, 128)
-        round_pair(nc.scalar.copy, 1, 256, 384)
+        round_pair(nc.vector.tensor_copy, 1, 256, 384)
+        round_pair(nc.scalar.copy, 1, 64, 128)
+        round_pair(nc.scalar.copy, 1, 128, 256)
+        round_pair(nc.scalar.copy, 1, 384, 448)
         round_pair(nc.scalar.copy, 1, 448, 512)
-        round_pair(nc.vector.tensor_copy, 1, 128, 256)
         second_product(0, 0, 128, nc.scalar.copy)
         store(0, 128)
-        round_pair(nc.vector.tensor_copy, 1, 384, 448)
         second_product(1, 128, 256, nc.scalar.copy)
         store(128, 256)
         second_product(2, 256, 384, nc.scalar.copy)

@@ -31,10 +31,9 @@ def tile_picked_posadd_none_l_kernel(tc, xT, w1, w2_words, w2_scales, pe, offs, 
         w2_sc = sb.tile([P, N], U8, name="w2_sc", align_bytes=64)
         nc.vector.memset(w2_sc[:].bitcast(I32), 0)
 
-        x_rows = xT.rearrange("(p u e) c -> u p e c", u=2, e=2)
-        x_pair = [sb.tile([P, 2, T], F32, name="x_pair%d" % u) for u in range(2)]
+        x_raw = sb.tile([P, PACK, T], F32, name="x_raw")
         pe_rows = pe.rearrange("(p t) c -> p t c", t=PACK)
-        pe_first = sb.tile([P, 2, T], F32, name="pe_first")
+        pe_first = sb.tile([P, 2, T], F32, name="pe_first", tag="pe_first")
         pe_third = sb.tile([P, T], F32, name="pe_third")
         pe_last = sb.tile([P, T], F32, name="pe_last")
 
@@ -42,8 +41,7 @@ def tile_picked_posadd_none_l_kernel(tc, xT, w1, w2_words, w2_scales, pe, offs, 
         nc.sync.dma_start(offsets[:], offs)
         for q in range(4):
             nc.sync.dma_start(w2_sc[32 * q : 32 * q + 4, :].bitcast(I32), w2_scales[0, 4 * q : 4 * q + 4, :].bitcast(I32))
-        for u in range(2):
-            nc.sync.dma_start(x_pair[u][:], x_rows[u])
+        nc.sync.dma_start(x_raw[:], xT.rearrange("(p j) c -> p j c", j=PACK))
         nc.sync.dma_start(pe_first[:], pe_rows[:, 0:2, :])
         nc.sync.dma_start(pe_third[:], pe_rows[:, 2, :])
         nc.sync.dma_start(pe_last[:], pe_rows[:, 3, :])
@@ -68,67 +66,70 @@ def tile_picked_posadd_none_l_kernel(tc, xT, w1, w2_words, w2_scales, pe, offs, 
             w1_sc.append(sb.tile([P, 2 * P], U8, name="w1_sc%d" % u, align_bytes=64))
             nc.vector.quantize_mx(out=w1_codes[u][:].bitcast(FP8X4), scales=w1_sc[u][:], in_=w1_bf[:])
 
-        acc = [ps.tile([P, S], F32, name="acc%d" % t, tag="bank%d" % t) for t in range(PACK)]
+        acc = [[ps.tile([P, HALF], F32, name="acc%d_%d" % (t, a), tag="bank%d" % (2 * t + a)) for a in range(2)] for t in range(PACK)]
         x_bf = sb.tile([P, S, PACK], BF16, name="x_bf", align_bytes=64)
-        x_picked = [sb.tile([P, 2, S], F32, name="x_picked%d" % u) for u in range(2)]
+        x_picked = sb.tile([P, PACK, S], F32, name="x_picked")
 
-        def pick_x(u, first, stop):
-            gather_on_vector(x_picked[u][:, 0, first:stop], x_pair[u][:, 0, :], first, stop)
-            gather_on_scalar(x_picked[u][:, 1, first:stop], x_pair[u][:, 1, :], first, stop)
+        def pick_x(gather, j, first, stop):
+            gather(x_picked[:, j, first:stop], x_raw[:, j, :], first, stop)
 
-        def round_x(u, first, stop):
-            nc.vector.tensor_copy(x_bf[:, first:stop, 2 * u : 2 * u + 2], x_picked[u][:, :, first:stop].rearrange("p e n -> p n e"))
+        def round_x(first, stop):
+            nc.vector.tensor_copy(x_bf[:, first:stop, :], x_picked[:, :, first:stop].rearrange("p j n -> p n j"))
 
-        pick_x(0, 0, S)
-        round_x(0, 0, S)
-        pick_x(1, 0, HALF)
-        pick_x(1, HALF, S)
-        round_x(1, 0, HALF)
-        round_x(1, HALF, S)
-        x_codes = [sb.tile([P, HALF], U32, name="x_codes%d" % a, align_bytes=64) for a in range(2)]
-        x_sc = [sb.tile([P, HALF], U8, name="x_sc%d" % a, align_bytes=64) for a in range(2)]
-        for a in range(2):
-            nc.vector.quantize_mx(
-                out=x_codes[a][:].bitcast(FP8X4),
-                scales=x_sc[a][:],
-                in_=x_bf[:, a * HALF : (a + 1) * HALF, :].rearrange("p n j -> p (n j)"),
-            )
-        for u in (1, 0):
-            for a in range(2):
-                for e in range(2):
-                    w1_cols = slice(e * P, (e + 1) * P)
-                    nc.tensor.matmul_mx(
-                        out=acc[2 * u + e][:, a * HALF : (a + 1) * HALF],
-                        lhsT=w1_codes[u][:, w1_cols].bitcast(FP8X4),
-                        lhsT_scale=w1_sc[u][:, w1_cols],
-                        rhs=x_codes[a][:].bitcast(FP8X4),
-                        rhs_scale=x_sc[a][:],
-                        start=True,
-                        stop=True,
-                    )
+        pick_x(gather_on_vector, 3, 0, HALF)
+        pick_x(gather_on_vector, 2, 0, HALF)
+        pick_x(gather_on_scalar, 0, 0, HALF)
+        pick_x(gather_on_scalar, 1, 0, HALF)
+        pick_x(gather_on_vector, 3, HALF, S)
+        for first in (256, 384):
+            for j in range(3):
+                pick_x(gather_on_scalar, j, first, first + 128)
+        round_x(0, HALF)
+        round_x(256, 384)
+        round_x(384, 512)
+        for first, stop, planes in ((0, 256, (2, 3, 1, 0)), (256, 384, (0, 1, 2, 3)), (384, 512, (0, 1, 2, 3))):
+            n = stop - first
+            x_codes = sb.tile([P, n], U32, name="x_codes%d" % first, align_bytes=64)
+            x_sc = sb.tile([P, n], U8, name="x_sc%d" % first, align_bytes=64)
+            nc.vector.quantize_mx(out=x_codes[:].bitcast(FP8X4), scales=x_sc[:], in_=x_bf[:, first:stop, :].rearrange("p n j -> p (n j)"))
+            for t in planes:
+                w1_cols = slice(t % 2 * P, (t % 2 + 1) * P)
+                nc.tensor.matmul_mx(
+                    out=acc[t][first // HALF][:, first % HALF : first % HALF + n],
+                    lhsT=w1_codes[t // 2][:, w1_cols].bitcast(FP8X4),
+                    lhsT_scale=w1_sc[t // 2][:, w1_cols],
+                    rhs=x_codes[:].bitcast(FP8X4),
+                    rhs_scale=x_sc[:],
+                    start=True,
+                    stop=True,
+                )
 
         picked = {t: sb.tile([P, S], F32, name="picked%d" % t, tag="picked%d" % t, align_bytes=64) for t in (0, 1, 3)}
         h = sb.tile([P, PACK, S], F32, name="h")
         h_bf = sb.tile([P, S, PACK], BF16, name="h_bf", align_bytes=64)
 
         def add(t, first, stop):
-            nc.vector.tensor_tensor(h[:, t, first:stop], acc[t][:, first:stop], picked[t][:, first:stop], ADD)
+            nc.vector.tensor_tensor(h[:, t, first:stop], acc[t][first // HALF][:, first % HALF : first % HALF + stop - first], picked[t][:, first:stop], ADD)
 
         def round_pair(copy, u, first, stop):
             copy(h_bf[:, first:stop, 2 * u : 2 * u + 2], h[:, 2 * u : 2 * u + 2, first:stop].rearrange("p e n -> p n e"))
 
         prod_late = sb.tile([P, 2, S], F32, name="prod_late")
         prod_third, prod_last = prod_late[:, 0, :], prod_late[:, 1, :]
-        nc.scalar.copy(out=prod_third, in_=acc[2][:])
-        nc.scalar.copy(out=prod_last[:, :HALF], in_=acc[3][:, :HALF])
+        nc.scalar.copy(out=prod_third[:, :HALF], in_=acc[2][0][:])
+        nc.scalar.copy(out=prod_last[:, :HALF], in_=acc[3][0][:])
+        gather_on_vector(picked[1][:, :384], pe_first[:, 1, :], 0, 384)
         for a in range(2):
             gather_on_scalar(picked[0][:, a * HALF : (a + 1) * HALF], pe_first[:, 0, :], a * HALF, (a + 1) * HALF)
-            gather_on_vector(picked[1][:, a * HALF : (a + 1) * HALF], pe_first[:, 1, :], a * HALF, (a + 1) * HALF)
+        gather_on_scalar(picked[1][:, 384:], pe_first[:, 1, :], 384, S)
+        prod_third_late = sb.tile([P, HALF], F32, name="prod_third_late", tag="pe_first")
+        nc.scalar.copy(out=prod_third_late[:], in_=acc[2][1][:])
         for a in range(2):
-            add(1, a * HALF, (a + 1) * HALF)
-            add(0, a * HALF, (a + 1) * HALF)
+            add(1 - a, a * HALF, (a + 1) * HALF)
+            add(a, a * HALF, (a + 1) * HALF)
             round_pair(nc.scalar.copy, 0, a * HALF, (a + 1) * HALF)
-        nc.vector.tensor_tensor(h[:, 2, :], pe_third[:].indirect(offsets[:]), prod_third, ADD)
+        nc.vector.tensor_tensor(h[:, 2, :HALF], pe_third[:].indirect(entries(0, HALF)), prod_third[:, :HALF], ADD)
+        nc.vector.tensor_tensor(h[:, 2, HALF:], pe_third[:].indirect(entries(HALF, S)), prod_third_late[:], ADD)
         w2_codes = sb.tile([P, N], U32, name="w2_codes", tag="picked1", align_bytes=64)
         nc.scalar.dma_start(w2_codes[:].bitcast(I32), w2_words[0].rearrange("p n t -> p (n t)").bitcast(I32))
 
@@ -139,7 +140,7 @@ def tile_picked_posadd_none_l_kernel(tc, xT, w1, w2_words, w2_scales, pe, offs, 
             h_codes = sb.tile([P, n], U32, name="h_codes%d" % c, align_bytes=64)
             h_sc = sb.tile([P, n], U8, name="h_sc%d" % c, align_bytes=64)
             nc.vector.quantize_mx(out=h_codes[:].bitcast(FP8X4), scales=h_sc[:], in_=h_bf[:, first:stop, :].rearrange("p n t -> p (n t)"))
-            res = ps.tile([P, n], F32, name="res%d" % c, tag="bank%d" % ((4 + c) % 8))
+            res = ps.tile([P, n], F32, name="res%d" % c, tag="bank%d" % c)
             nc.tensor.matmul_mx(
                 out=res[:],
                 lhsT=w2_codes[:].bitcast(FP8X4),
@@ -170,7 +171,8 @@ def tile_picked_posadd_none_l_kernel(tc, xT, w1, w2_words, w2_scales, pe, offs, 
         round_pair(nc.scalar.copy, 1, 384, 448)
         round_pair(nc.scalar.copy, 1, 448, 512)
         second_product(0, 0, 128, nc.scalar.copy)
-        store(0, 128)
+        store(0, 64)
+        store(64, 128)
         second_product(1, 128, 256, nc.scalar.copy)
         store(128, 256)
         second_product(2, 256, 384, nc.scalar.copy)

@@ -131,7 +131,8 @@ def tile_picked_posadd_none_l_kernel(tc, xT, w1, w2_words, w2_scales, pe, offs, 
         nc.vector.tensor_tensor(h[:, 2, :HALF], pe_third[:].indirect(entries(0, HALF)), prod_third[:, :HALF], ADD)
         nc.vector.tensor_tensor(h[:, 2, HALF:], pe_third[:].indirect(entries(HALF, S)), prod_third_late[:], ADD)
         w2_codes = sb.tile([P, N], U32, name="w2_codes", tag="picked1", align_bytes=64)
-        nc.scalar.dma_start(w2_codes[:].bitcast(I32), w2_words[0].rearrange("p n t -> p (n t)").bitcast(I32))
+        for queue, rows in ((nc.sync, slice(0, 64)), (nc.scalar, slice(64, P))):
+            queue.dma_start(w2_codes[rows, :].bitcast(I32), w2_words[0, rows].rearrange("p n t -> p (n t)").bitcast(I32))
 
         res_sb = sb.tile([P, S], F32, name="res_sb")
 
@@ -171,8 +172,7 @@ def tile_picked_posadd_none_l_kernel(tc, xT, w1, w2_words, w2_scales, pe, offs, 
         round_pair(nc.scalar.copy, 1, 384, 448)
         round_pair(nc.scalar.copy, 1, 448, 512)
         second_product(0, 0, 128, nc.scalar.copy)
-        store(0, 64)
-        store(64, 128)
+        store(0, 128)
         second_product(1, 128, 256, nc.scalar.copy)
         store(128, 256)
         second_product(2, 256, 384, nc.scalar.copy)

@@ -39,8 +39,9 @@ def tile_picked_posadd_none_l_kernel(tc, xT, w1, w2_words, w2_scales, pe, offs, 
 
         nc.sync.dma_start(w1_raw[:], w1.rearrange("(p j) c -> p j c", j=PACK))
         nc.sync.dma_start(offsets[:], offs)
-        for q in range(4):
-            nc.sync.dma_start(w2_sc[32 * q : 32 * q + 4, :].bitcast(I32), w2_scales[0, 4 * q : 4 * q + 4, :].bitcast(I32))
+        for row, count in ((0, 2), (2, 2), (4, 4), (8, 4), (12, 4)):
+            first = 32 * (row // 4) + row % 4
+            nc.sync.dma_start(w2_sc[first : first + count, :].bitcast(I32), w2_scales[0, row : row + count, :].bitcast(I32))
         nc.sync.dma_start(x_raw[:], xT.rearrange("(p j) c -> p j c", j=PACK))
         nc.sync.dma_start(pe_first[:], pe_rows[:, 0:2, :])
         nc.sync.dma_start(pe_third[:], pe_rows[:, 2, :])
@@ -131,8 +132,7 @@ def tile_picked_posadd_none_l_kernel(tc, xT, w1, w2_words, w2_scales, pe, offs, 
         nc.vector.tensor_tensor(h[:, 2, :HALF], pe_third[:].indirect(entries(0, HALF)), prod_third[:, :HALF], ADD)
         nc.vector.tensor_tensor(h[:, 2, HALF:], pe_third[:].indirect(entries(HALF, S)), prod_third_late[:], ADD)
         w2_codes = sb.tile([P, N], U32, name="w2_codes", tag="picked1", align_bytes=64)
-        for queue, rows in ((nc.sync, slice(0, 64)), (nc.scalar, slice(64, P))):
-            queue.dma_start(w2_codes[rows, :].bitcast(I32), w2_words[0, rows].rearrange("p n t -> p (n t)").bitcast(I32))
+        nc.scalar.dma_start(w2_codes[:].bitcast(I32), w2_words[0].rearrange("p n t -> p (n t)").bitcast(I32))
 
         res_sb = sb.tile([P, S], F32, name="res_sb")
 

from contextlib import ExitStack

import concourse.mybir as mybir

K, T, S, H, N = 512, 2048, 512, 512, 128
FLOPS = 2 * K * H * S + 2 * H * N * S

F32 = mybir.dt.float32
BF16 = mybir.dt.bfloat16
I32 = mybir.dt.int32
U32 = mybir.dt.uint32
U16 = mybir.dt.uint16
U8 = mybir.dt.uint8
FP8X4 = mybir.dt.float8_e4m3fn_x4
ADD = mybir.AluOpType.add
COPY = mybir.ActivationFunctionType.Copy

P = 128
PACK = 4
HALF = S // 2


def tile_picked_posadd_none_l_kernel(tc, xT, w1, w2_words, w2_scales, pe, offs, out):
    nc = tc.nc
    with ExitStack() as ctx:
        sb = ctx.enter_context(tc.tile_pool(name="sb", bufs=1))
        ps = ctx.enter_context(tc.psum_pool(name="ps", bufs=1))

        offsets = sb.tile([P, S // 16], U16, name="offsets")
        w1_raw = sb.tile([P, PACK, H], F32, name="w1_raw")
        w2_sc = sb.tile([P, N], U8, name="w2_sc", align_bytes=64)
        nc.vector.memset(w2_sc[:].bitcast(I32), 0)

        x_raw = sb.tile([P, PACK, T], F32, name="x_raw")
        pe_rows = pe.rearrange("(p t) c -> p t c", t=PACK)
        pe_first = sb.tile([P, 2, T], F32, name="pe_first", tag="pe_first")
        pe_third = sb.tile([P, T], F32, name="pe_third")
        pe_last = sb.tile([P, T], F32, name="pe_last")

        nc.sync.dma_start(w1_raw[:], w1.rearrange("(p j) c -> p j c", j=PACK))
        nc.sync.dma_start(offsets[:], offs)
        for row, count in ((0, 2), (2, 2), (4, 4), (8, 4), (12, 4)):
            first = 32 * (row // 4) + row % 4
            nc.sync.dma_start(w2_sc[first : first + count, :].bitcast(I32), w2_scales[0, row : row + count, :].bitcast(I32))
        nc.sync.dma_start(x_raw[:], xT.rearrange("(p j) c -> p j c", j=PACK))
        nc.sync.dma_start(pe_first[:], pe_rows[:, 0:2, :])
        nc.sync.dma_start(pe_third[:], pe_rows[:, 2, :])
        nc.sync.dma_start(pe_last[:], pe_rows[:, 3, :])

        def entries(first, stop):
            return offsets[:, first // 16 : stop // 16]

        def gather_on_vector(dst, window, first, stop):
            nc.vector.tensor_copy(dst, window.indirect(entries(first, stop)))

        def gather_on_scalar(dst, window, first, stop):
            nc.scalar.activation(dst, window.indirect(entries(first, stop)), COPY)

        w1_codes, w1_sc = [], []
        for u in range(2):
            w1_bf = sb.tile([P, 2 * P * PACK], BF16, name="w1_bf%d" % u, align_bytes=64)
            nc.scalar.copy(
                out=w1_bf[:].rearrange("p (e m j) -> p m j e", e=2, j=PACK),
                in_=w1_raw[:].rearrange("p j (m t) -> p m j t", t=PACK)[:, :, :, 2 * u : 2 * u + 2],
            )
            w1_codes.append(sb.tile([P, 2 * P], U32, name="w1_codes%d" % u, align_bytes=64))
            w1_sc.append(sb.tile([P, 2 * P], U8, name="w1_sc%d" % u, align_bytes=64))
            nc.vector.quantize_mx(out=w1_codes[u][:].bitcast(FP8X4), scales=w1_sc[u][:], in_=w1_bf[:])

        acc = [[ps.tile([P, HALF], F32, name="acc%d_%d" % (t, a), tag="bank%d" % (2 * t + a)) for a in range(2)] for t in range(PACK)]
        x_bf = sb.tile([P, S, PACK], BF16, name="x_bf", align_bytes=64)
        x_picked = sb.tile([P, PACK, S], F32, name="x_picked")

        def pick_x(gather, j, first, stop):
            gather(x_picked[:, j, first:stop], x_raw[:, j, :], first, stop)

        def round_x(first, stop):
            nc.vector.tensor_copy(x_bf[:, first:stop, :], x_picked[:, :, first:stop].rearrange("p j n -> p n j"))

        pick_x(gather_on_vector, 3, 0, HALF)
        pick_x(gather_on_vector, 2, 0, HALF)
        pick_x(gather_on_scalar, 0, 0, HALF)
        pick_x(gather_on_scalar, 1, 0, HALF)
        pick_x(gather_on_vector, 3, HALF, S)
        for first in (256, 384):
            for j in range(3):
                pick_x(gather_on_scalar, j, first, first + 128)
        round_x(0, HALF)
        round_x(256, 384)
        round_x(384, 512)
        for first, stop, planes in ((0, 256, (2, 3, 1, 0)), (256, 384, (0, 1, 2, 3)), (384, 512, (0, 1, 2, 3))):
            n = stop - first
            x_codes = sb.tile([P, n], U32, name="x_codes%d" % first, align_bytes=64)
            x_sc = sb.tile([P, n], U8, name="x_sc%d" % first, align_bytes=64)
            nc.vector.quantize_mx(out=x_codes[:].bitcast(FP8X4), scales=x_sc[:], in_=x_bf[:, first:stop, :].rearrange("p n j -> p (n j)"))
            for t in planes:
                w1_cols = slice(t % 2 * P, (t % 2 + 1) * P)
                nc.tensor.matmul_mx(
                    out=acc[t][first // HALF][:, first % HALF : first % HALF + n],
                    lhsT=w1_codes[t // 2][:, w1_cols].bitcast(FP8X4),
                    lhsT_scale=w1_sc[t // 2][:, w1_cols],
                    rhs=x_codes[:].bitcast(FP8X4),
                    rhs_scale=x_sc[:],
                    start=True,
                    stop=True,
                )

        picked = {t: sb.tile([P, S], F32, name="picked%d" % t, tag="picked%d" % t, align_bytes=64) for t in (0, 1, 3)}
        h = sb.tile([P, PACK, S], F32, name="h")
        h_bf = sb.tile([P, S, PACK], BF16, name="h_bf", align_bytes=64)

        def add(t, first, stop):
            nc.vector.tensor_tensor(h[:, t, first:stop], acc[t][first // HALF][:, first % HALF : first % HALF + stop - first], picked[t][:, first:stop], ADD)

        def round_pair(copy, u, first, stop):
            copy(h_bf[:, first:stop, 2 * u : 2 * u + 2], h[:, 2 * u : 2 * u + 2, first:stop].rearrange("p e n -> p n e"))

        prod_late = sb.tile([P, 2, S], F32, name="prod_late")
        prod_third, prod_last = prod_late[:, 0, :], prod_late[:, 1, :]
        nc.scalar.copy(out=prod_third[:, :HALF], in_=acc[2][0][:])
        nc.scalar.copy(out=prod_last[:, :HALF], in_=acc[3][0][:])
        gather_on_vector(picked[1][:, :384], pe_first[:, 1, :], 0, 384)
        for a in range(2):
            gather_on_scalar(picked[0][:, a * HALF : (a + 1) * HALF], pe_first[:, 0, :], a * HALF, (a + 1) * HALF)
        gather_on_scalar(picked[1][:, 384:], pe_first[:, 1, :], 384, S)
        prod_third_late = sb.tile([P, HALF], F32, name="prod_third_late", tag="pe_first")
        nc.scalar.copy(out=prod_third_late[:], in_=acc[2][1][:])
        for a in range(2):
            add(1 - a, a * HALF, (a + 1) * HALF)
            add(a, a * HALF, (a + 1) * HALF)
            round_pair(nc.scalar.copy, 0, a * HALF, (a + 1) * HALF)
        nc.vector.tensor_tensor(h[:, 2, :HALF], pe_third[:].indirect(entries(0, HALF)), prod_third[:, :HALF], ADD)
        nc.vector.tensor_tensor(h[:, 2, HALF:], pe_third[:].indirect(entries(HALF, S)), prod_third_late[:], ADD)
        w2_codes = sb.tile([P, N], U32, name="w2_codes", tag="picked1", align_bytes=64)
        nc.scalar.dma_start(w2_codes[:].bitcast(I32), w2_words[0].rearrange("p n t -> p (n t)").bitcast(I32))

        res_sb = sb.tile([P, S], F32, name="res_sb")

        def second_product(c, first, stop, copy):
            n = stop - first
            h_codes = sb.tile([P, n], U32, name="h_codes%d" % c, align_bytes=64)
            h_sc = sb.tile([P, n], U8, name="h_sc%d" % c, align_bytes=64)
            nc.vector.quantize_mx(out=h_codes[:].bitcast(FP8X4), scales=h_sc[:], in_=h_bf[:, first:stop, :].rearrange("p n t -> p (n t)"))
            res = ps.tile([P, n], F32, name="res%d" % c, tag="bank%d" % c)
            nc.tensor.matmul_mx(
                out=res[:],
                lhsT=w2_codes[:].bitcast(FP8X4),
                lhsT_scale=w2_sc[:],
                rhs=h_codes[:].bitcast(FP8X4),
                rhs_scale=h_sc[:],
                start=True,
                stop=True,
            )
            copy(res_sb[:, first:stop], res[:])

        def store(first, stop, queue=nc.sync):
            queue.dma_start(out[:, first:stop], res_sb[:, first:stop])

        def fused(first, stop):
            nc.vector.tensor_tensor(h[:, 3, first:stop], pe_last[:].indirect(entries(first, stop)), prod_last[:, first:stop], ADD)

        gather_on_scalar(picked[3][:, 256:384], pe_last[:], 256, 384)
        gather_on_scalar(picked[3][:, 384:512], pe_last[:], 384, 512)
        fused(0, 128)
        fused(128, 256)
        add(3, 256, 384)
        round_pair(nc.vector.tensor_copy, 1, 0, 64)
        add(3, 384, 512)
        round_pair(nc.vector.tensor_copy, 1, 256, 384)
        round_pair(nc.scalar.copy, 1, 64, 128)
        round_pair(nc.scalar.copy, 1, 128, 256)
        round_pair(nc.scalar.copy, 1, 384, 448)
        round_pair(nc.scalar.copy, 1, 448, 512)
        second_product(0, 0, 128, nc.scalar.copy)
        store(0, 128)
        second_product(1, 128, 256, nc.scalar.copy)
        store(128, 256)
        second_product(2, 256, 384, nc.scalar.copy)
        store(256, 384, nc.scalar)
        second_product(3, 384, 448, nc.vector.tensor_copy)
        second_product(4, 448, 512, nc.vector.tensor_copy)
        store(384, 512)
